import numpy as np, ml_dtypes
CORES = [9,25,41,57]
N = 4
BF = ml_dtypes.bfloat16
T, R, S, H, CAP = 512, 64, 8, 4096, 2048
U, A, M, B0 = T // R, CAP // 16, max(T, CAP // 4), ((H + 1) << S) // 8191 + 1
def keys(x, hc):
    X = np.ascontiguousarray(x.transpose(1, 0, 2)).reshape(128, N * T).astype(np.int64); h = hc[0].astype(np.int64)
    before = np.concatenate([np.zeros((128, 1), np.int64), X[:, :-1]], axis=1)
    return X, ((h[:, :1] * before + h[:, 1:] * X) >> S) & (H - 1)
def stretches(v):
    return np.ascontiguousarray(v.reshape(128, N, T).transpose(1, 0, 2)).astype(np.float32)
def multipliers(rng):
    return np.stack([rng.integers(1, 1024, 128), rng.integers(B0, (1 << S) + 1, 128)], axis=1)
def keyset(rng, n):
    return np.argsort(rng.random((128, n)), axis=-1)[:, :M]
def pools(rng, K):
    return np.take_along_axis(np.broadcast_to(K, (N,) + K.shape), np.argsort(rng.random((N,) + K.shape), axis=-1), axis=-1)
def counts(rng):
    d = rng.integers(0, A - R + 1, (N, 64)); return np.stack([A + d, A - d], axis=2).reshape(N, 128)
def uneven(rng, n):
    v = np.concatenate([[T], R + n // 15 + (np.arange(15) < n % 15)])
    return rng.permuted(np.broadcast_to(v, (N, 8, 16)).copy(), axis=-1).reshape(N, 128)
def order(rng, D, P, pin=False):
    i = np.arange(P.shape[-1]); e = rng.random((N, 128, U, P.shape[-1]), dtype=np.float32)
    b = rng.permuted(np.broadcast_to(np.arange(U), (N, 128, U)).copy(), axis=-1)[..., None]
    e = e - (i // R == b) + 4 * (i >= D[:, :, None, None])
    if pin: e[..., 0] = -9; e[..., 1] = -8
    o = np.argsort(e, axis=-1)[..., :R]
    if pin: o = np.concatenate([o[..., :1], rng.permuted(o[..., 2:], axis=-1), o[..., 1:2]], axis=-1)
    else: o = rng.permuted(o, axis=-1)
    return np.take_along_axis(np.broadcast_to(P[:, :, None], (N, 128, U, P.shape[-1])), o, axis=-1).reshape(N, 128, T)
def spell(rng, k, h):
    kk = k.transpose(1, 0, 2).reshape(128, N * T).astype(np.int64); X = np.zeros((128, N * T), np.int64); coin = rng.random((128, N * T)); up = rng.random((128, N * T)) < 0.5; last = np.zeros(128, np.int64); a, b = h[:, 0], h[:, 1]
    for t in range(N * T):
        w = ((kk[:, t] << S) - a * last) & ((H << S) - 1); w2 = w + (H << S)
        w = np.where(up[:, t] & ((w2 + (1 << S) - 1) // b <= 8191), w2, w); lo = (w + b - 1) // b; hi = (w + (1 << S) - 1) // b
        last = lo + np.floor(coin[:, t] * (hi - lo + 1)).astype(np.int64); X[:, t] = last
    return {"x": np.ascontiguousarray(X.reshape(128, N, T).transpose(1, 0, 2)).astype(np.int32), "hc": np.broadcast_to(h, (N, 128, 2)).astype(np.int32)}
def setup_inputs(rng):
    D = np.maximum(R, counts(rng) - rng.integers(0, 5, (N, 128)))
    return spell(rng, order(rng, D, pools(rng, keyset(rng, H))), multipliers(rng))
def setup_inputs_full(rng):
    D = np.where(np.arange(128) // 16 % 2 == 0, uneven(rng, CAP - T - 15 * R), counts(rng))
    P = pools(rng, keyset(rng, H)); P[:, ::3] = np.stack([keyset(rng, H)[::3] for r in range(N)])
    return spell(rng, order(rng, D, P), multipliers(rng))
def setup_inputs_ends(rng):
    P = pools(rng, keyset(rng, H - 2) + 1); P[..., 0] = 0; P[..., 1] = H - 1
    k = order(rng, counts(rng), P, True).reshape(N, 128, U, R); k[:, ::2, 1::2, 0] = H - 1; k[:, ::2, 1::2, R - 1] = 0
    k[0, 1::4, 0, R - 1] = k[0, 1::4, 0, 1]; k[0, 1::4, 0, 0] = H - 1; k[0, 1::4, 0, 1] = 0
    h = multipliers(rng); h[1::4, 0] = 0
    d = spell(rng, k.reshape(N, 128, T), h); d["x"][0, 1::4, 1] = 0; return d
def setup_inputs_far(rng):
    K = keyset(rng, H); P = pools(rng, K[:, M // 2:]); Q = pools(rng, K[:, :M // 2]); P[0] = Q[0]; P[N - 1] = Q[N - 1]; P[N - 1, ::2] = Q[0, ::2]
    D = counts(rng); D[N - 1] = D[0]
    return spell(rng, order(rng, D, P), multipliers(rng))
def setup_inputs_same(rng):
    K = keyset(rng, H); k = order(rng, np.full((N, 128), R), np.broadcast_to(K, (N,) + K.shape))
    k[:, 1::2] = np.tile(k[0, 1::2, :R], (1, U)); return spell(rng, k, multipliers(rng))
def setup_inputs_spread(rng):
    K = (rng.integers(0, H, (128, 1)) + np.arange(M)) % H
    h = np.stack([rng.choice(np.array([0, 1, 1023]), 128), rng.choice(np.array([B0, 1 << S]), 128)], axis=1)
    return spell(rng, order(rng, uneven(rng, 0), pools(rng, K)), h)
def check_inputs(d):
    bad = []; x, hc = d["x"], d["hc"]
    if not (x.min() >= 0 and x.max() <= 8191): bad.append("tokens")
    if not (hc[..., 0].min() >= 0 and hc[..., 0].max() <= 1023 and hc[..., 1].min() >= 1 and hc[..., 1].max() <= 1 << S): bad.append("multipliers")
    if (hc != hc[:1]).any(): bad.append("hc_alike")
    k = keys(x, hc)[1].reshape(128, N, T).transpose(1, 0, 2)
    s = np.sort(k.reshape(N, 128, U, R), axis=-1)
    if (s[..., 1:] == s[..., :-1]).any(): bad.append("runs")
    s = np.sort(k, axis=-1); n = 1 + np.sum(s[..., 1:] != s[..., :-1], axis=-1)
    if np.sum(n.reshape(N, 8, 16), axis=-1).max() > CAP: bad.append("new_keys")
    return bad
def reference(x, hc):
    X, k = keys(x, hc); L = N * T
    u = (np.arange(128)[:, None] * H + k).reshape(-1); o = np.argsort(u, kind="stable")
    same = u[o[1:]] == u[o[:-1]]
    prev = np.full(128 * L, -1, np.int64); prev[o[1:][same]] = o[:-1][same] % L
    prev = prev.reshape(128, L); after = np.where(prev >= 0, np.take_along_axis(X, prev + 1, axis=1), -1)
    return {"y": stretches(prev), "z": stretches(after)}

@@ -1,0 +1,364 @@
+from concourse.bass import DstId, RemoteDMATransfer
+from concourse.mybir import AluOpType, ActivationFunctionType
+
+N, TT, R, H, S = 4, 512, 64, 4096, 8
+W = R + 2
+EW, FW = 145, 135
+EMPTY = 32.0
+PIECES = [(0, 0, 512), (1, 0, 512), (2, 0, 512), (3, 0, 256), (3, 256, 128), (3, 384, 128)]
+
+SCRATCH = {
+    "xq": ("sbuf", [128, 8, W], "int32"),
+    "xr": ("sbuf", [128, N, 2, W], "int32"),
+    "hq": ("sbuf", [128, 16], "int32"),
+    "hf": ("sbuf", [128, 8], "float32"),
+    "hb": ("sbuf", [128, N, 2, W], "bfloat16"),
+    "lb": ("sbuf", [128, N, 2, W], "bfloat16"),
+    "dk": ("sbuf", [128, 128], "bfloat16"),
+    "dg": ("sbuf", [128, 8, 128], "float16"),
+    "d0": ("sbuf", [128, 4, 128], "float16"),
+    "em": ("sbuf", [128, 8, EW], "bfloat16"),
+    "fm": ("sbuf", [128, 4, FW], "bfloat16"),
+    "cm": ("sbuf", [128, N, 128], "bfloat16"),
+    "ct": ("sbuf", [128, TT], "bfloat16"),
+    "c32": ("sbuf", [128, 1024], "bfloat16"),
+    "eb": ("sbuf", [128, 1], "float32"),
+    "kt": ("sbuf", [128, TT], "float32"),
+    "ki": ("sbuf", [128, TT], "int32"),
+    "kj": ("sbuf", [128, N, 4, 32], "int32"),
+    "off": ("sbuf", [128, TT], "uint16"),
+    "val": ("sbuf", [128, N * TT], "float32"),
+    "tab0": ("sbuf", [128, H], "bfloat16"),
+    "tab1": ("sbuf", [128, H], "bfloat16"),
+    "tab2": ("sbuf", [128, H], "float32"),
+    "tab3": ("sbuf", [128, H], "float32"),
+    "got0": ("sbuf", [128, N * TT], "bfloat16"),
+    "got1": ("sbuf", [128, N * TT], "bfloat16"),
+    "got2": ("sbuf", [128, N * TT], "bfloat16"),
+    "got3": ("sbuf", [128, N * TT], "bfloat16"),
+    "outb": ("sbuf", [128, N, 256], "float32"),
+    "land": ("sbuf", [128, N, 256], "float32"),
+    "kp0": ("psum", [128, 4, 4, 2, 16], "float32"),
+    "kp1": ("psum", [128, 4, 4, 2, 16], "float32"),
+    "vp0": ("psum", [128, 512], "float32"),
+    "vp1": ("psum", [128, 512], "float32"),
+    "vp2": ("psum", [128, 512], "float32"),
+    "vp3": ("psum", [128, 512], "float32"),
+    "rp0": ("psum", [128, 512], "float32"),
+    "rp1": ("psum", [128, 512], "float32"),
+}
+SEMAPHORES = (["ld", "ldh", "cz", "c32", "gk", "ge", "gf", "gct", "cs_z", "cs_m", "tv", "ts", "tg", "hf", "dz", "dg",
+               "gi", "eb", "dgo", "dg0", "dgr", "kp0", "kp1", "k0", "k1", "sent", "sta", "stb"]
+              + ["ch%d" % i for i in range(4)] + ["arr%d" % i for i in range(N)]
+              + ["vp%d" % i for i in range(5)] + ["vc%d" % i for i in range(5)]
+              + ["rp%d" % i for i in range(6)] + ["ev%d" % i for i in range(6)]
+              + ["res%d_%d" % (d, i) for d in range(N) for i in range(3)])
+
+
+def rank_program(g, core, T, topo):
+    d = T.rank_of(core)
+    if d is None:
+        return
+    A, F = AluOpType, ActivationFunctionType
+    V, SC, PE, SY = g.vector, g.scalar, g.tensor, g.sync
+    Q = {"g": g, "v": V, "s": SC, "p": PE, "y": SY}
+    cnt, seen, top = {}, {}, {}
+
+    def inc(ins, name, n=1):
+        ins.then_inc(T.sem[name], n)
+        cnt[name] = cnt.get(name, 0) + n
+
+    def wait(q, name, n):
+        if seen.get((q, name), 0) < n:
+            Q[q].wait_ge(T.sem[name], n)
+            seen[(q, name)] = n
+            top[name] = max(top.get(name, 0), n)
+
+    tab = [T.tab0, T.tab1, T.tab2, T.tab3]
+    got = [T.got0, T.got1, T.got2, T.got3]
+    vpb = [T.vp0, T.vp1, T.vp2, T.vp3]
+    others = [r for r in range(N) if r != d]
+
+    def split(src, dst_ranks):
+        e = topo.engines(T.cores[src], T.cores[dst_ranks[0]])
+        ev, od = e[0::2], e[1::2]
+        sets = [ev[:len(ev) // 2], ev[len(ev) // 2:], od]
+        return {r: sets[i] for i, r in enumerate(dst_ranks)}
+
+    def bits(es):
+        return sum(1 << e for e in es)
+
+    for u in range(8):
+        q = SY if u % 2 == 0 else SC
+        if u == 0:
+            inc(q.dma_start(T.xq[0::8, :, 2:W], T.x[:, 0:R]), "ld", 16)
+        else:
+            inc(q.dma_start(T.xq[u::8, :, :], T.x[:, R * u - 2:R * u + R]), "ld", 16)
+    inc(SY.dma_start(T.xq[0::8, :, 0:2], T.x[:, TT - 2:TT]), "ld", 16)
+    for u in range(8):
+        inc(SY.dma_start(T.hq[u::8, :], T.hc[:, :]), "ldh", 16)
+    LD, LDH = cnt["ld"], cnt["ldh"]
+
+    inc(g.iota(T.ct[32:64, :], [[1, 8], [0, R]], int(EMPTY), 0, allow_small_or_imprecise_dtypes=True), "gct")
+    inc(g.iota(T.ct[0:32, :], [[0, 8], [1, R]], int(EMPTY), 0, allow_small_or_imprecise_dtypes=True), "gct")
+    wait("g", "gct", 2)
+    inc(g.iota(T.dk[:, :], [[1, 128]], 0, -1, allow_small_or_imprecise_dtypes=True), "gk")
+    wait("g", "cz", 2)
+    for a in range(4):
+        v = T.em[:, :, 17 + 32 * a:17 + 32 * a + 13:4]
+        inc(g.affine_select(v, v, [[-1, 8], [-8, 4]], A.not_equal, 1.0, -32 * a, 1), "ge")
+    wait("g", "ld", LD)
+    masks = split(d, others)
+    tr = []
+    for r in others:
+        rid, pid, _ = topo.addr(T.cores[r])
+        tr.append(RemoteDMATransfer(dst_ids=[DstId(rid=rid, pnc=pid)], dma_engine_mask=bits(masks[r]),
+                                    remote_sem=T.sem["arr%d" % d], src=T.xq[:, 2 * r:2 * r + 2, :], dst=T.xr[:, d, :, :]))
+        cnt["sent"] = cnt.get("sent", 0) + len(masks[r])
+    g.remote_dma_fused(tr, local_sem=T.sem.sent)
+    arr = {r: len(split(r, [o for o in range(N) if o != r])[d]) for r in others}
+    inc(g.iota(T.tab3[:, 3072:4096], [[0, 1024]], int(EMPTY), 0, allow_small_or_imprecise_dtypes=True), "tg")
+    fy, fz = T.fm[:, :, 7:64:8], T.fm[:, :, 71:128:8]
+    inc(g.affine_select(fy, fy, [[0, 4], [-16, 2], [-32, 4]], A.not_equal, 64.0, -2, 1), "gf")
+    inc(g.affine_select(fz, fz, [[-4, 4], [-16, 2], [-32, 4]], A.not_equal, 1.0, 0, 1), "gf")
+    wait("g", "gf", 2)
+    inc(g.affine_select(fy, fy, [[0, 4], [-16, 2], [-32, 4]], A.not_equal, 1.0, -3, 1), "gf")
+    inc(g.affine_select(fz, fz, [[-4, 4], [-16, 2], [-32, 4]], A.not_equal, -1.0, -1, 1), "gf")
+
+    def digits(rs, name):
+        for r in rs:
+            if r == d:
+                wait("v", "ld", LD)
+            else:
+                wait("v", "arr%d" % r, arr[r])
+            src = T.xq[:, 2 * d:2 * d + 2, :] if r == d else T.xr[:, r, :, :]
+            inc(V.tensor_scalar(T.hb[:, r, :, :], src, 64.0, None, A.add), name)
+        yield
+        wait("v", name, len(rs))
+        for r in rs:
+            src = T.xq[:, 2 * d:2 * d + 2, :] if r == d else T.xr[:, r, :, :]
+            inc(V.tensor_tensor(T.lb[:, r, :, :], T.hb[:, r, :, :], src, A.subtract), name)
+        yield
+
+    def keys(r0, r1, kp, kpn, name):
+        n, c0, c1 = r1 - r0, 128 * r0, 128 * r1
+        wait("v", kpn, 2 * n)
+        inc(V.transpose(T.kt[:, c0:c1], kp[:, 0:n, :, :, :]), name)
+        yield
+        wait("v", name, 1)
+        inc(V.tensor_copy(T.ki[:, c0:c1], T.kt[:, c0:c1]), name)
+        yield
+        wait("v", name, 2)
+        inc(V.tensor_scalar(T.kj[:, r0:r1, :, :], T.ki[:, c0:c1], S, H - 1, A.logical_shift_right, A.bitwise_and), name)
+        yield
+        wait("v", name, 3)
+        for c in range(4):
+            inc(V.tensor_copy(T.off[:, c0 + c:c1:4], T.kj[:, r0:r1, c, :]), name)
+        yield
+
+    inc(V.memset(T.c32[:, :], EMPTY), "c32")
+    inc(V.memset(T.em[:, :, :], 0.0), "cz")
+    inc(V.memset(T.fm[:, :, :], 0.0), "cz")
+    inc(V.memset(T.cm[:, :, :], 0.0), "cs_z")
+    inc(V.memset(T.d0[:, :, :], 0.0), "dz")
+    inc(V.memset(T.tab0[:, :], EMPTY), "tv")
+    wait("v", "cs_z", 1)
+    inc(V.memset(T.cm[0:1, :, 3::16], 1.0), "cs_m")
+    inc(V.memset(T.cm[32:33, :, 2::16], 1.0), "cs_m")
+    inc(V.memset(T.cm[64:65, :, 1::4], -1.0), "cs_m")
+    for r in range(1, N):
+        inc(V.memset(T.cm[64:65, r, 2::16], 8.0 * r), "cs_m")
+    inc(V.memset(T.ct[64:65, :], 1.0), "cs_m")
+    CSM = cnt["cs_m"]
+    if d != 0:
+        for _ in digits([d], "dgo"):
+            pass
+    wait("v", "ldh", LDH)
+    inc(V.tensor_copy(T.hf[:, 0:4], T.hq[:, 4 * d:4 * d + 4]), "hf")
+    inc(V.tensor_scalar(T.hf[:, 4:8], T.hq[:, 4 * d:4 * d + 4], -1.0, None, A.mult), "hf")
+    for s in range(4):
+        inc(V.memset(got[s][:, 0:R], EMPTY), "gi")
+    inc(V.memset(T.eb[0:64, :], -(65.0 * EMPTY + 1.0)), "eb")
+    inc(V.memset(T.eb[64:128, :], -1.0), "eb")
+    wait("v", "hf", 2)
+    wait("v", "gk", 1)
+    wait("v", "dz", 1)
+    for i in range(8):
+        inc(V.tensor_scalar(T.dg[:, i, :], T.dk[:, :], 0.0, T.hf[:, i:i + 1], A.is_equal, A.mult), "dg")
+    for i in range(4):
+        inc(V.tensor_scalar(T.d0[:, i, 0::8], T.dk[:, 0::8], 0.0, T.hf[:, 2 * i:2 * i + 1], A.is_equal, A.mult), "dg")
+    inc(V.memset(T.tab1[:, :], EMPTY), "tv")
+    for _ in digits([0], "dg0"):
+        pass
+    for _ in keys(0, 1, T.kp0, "kp0", "k0"):
+        pass
+    rest = [r for r in range(1, N) if r != d]
+
+    items = ([(d, 0, 8)] if d != 0 else []) + [(0, 0, 3), (0, 3, 8)] + [(r, 0, 8) for r in rest]
+    need = {}
+    for i, (r, u0, u1) in enumerate(items):
+        for u in range(u0, u1):
+            need[8 * r + u] = i
+
+    def keysum(r, kp, slot, name):
+        for e in range(2):
+            out = kp[:, slot, :, e, :]
+            one = kp[:, slot, 0, e, 0:1]
+            pa, pb, na, nb = T.dg[:, 2 * e, :], T.dg[:, 2 * e + 1, :], T.dg[:, 4 + 2 * e, :], T.dg[:, 5 + 2 * e, :]
+            p0, n0 = T.d0[:, e, :], T.d0[:, 2 + e, :]
+            ms = [(out, pb, T.hb[:, r, e, 2:W]), (out, pa, T.hb[:, r, e, 1:W - 1]),
+                  (out, nb, T.lb[:, r, e, 2:W]), (out, na, T.lb[:, r, e, 1:W - 1]),
+                  (one, n0, T.hb[:, r, e, 1:2]), (one, p0, T.lb[:, r, e, 1:2])]
+            if r > 0:
+                ms += [(one, p0, T.hb[:, r - 1, e, 1:2]), (one, n0, T.lb[:, r - 1, e, 1:2])]
+            for i, (o, l, x) in enumerate(ms):
+                ins = PE.matmul(o, l, x, i == 0, i == len(ms) - 1)
+            inc(ins, name)
+
+    def spread(i):
+        r, u0, u1 = items[i]
+        bank = vpb[i % 4]
+        if i >= 4:
+            wait("p", "vc%d" % (i - 4), 1)
+        wait("p", "ge", 4)
+        wait("p", "gct", 2)
+        wait("p", "cs_m", CSM)
+        PE.matmul(bank[:, 0:R * (u1 - u0)], T.cm[0:65, r, :], T.ct[0:65, R * u0:R * u1], True, False)
+        for u in range(u0, u1):
+            for e in range(2):
+                for j, src in enumerate((T.hb, T.lb)):
+                    o = 17 - 16 * e - j
+                    last = u == u1 - 1 and e == 1 and j == 1
+                    ins = PE.matmul(bank[:, R * (u - u0):R * (u - u0 + 1)], T.em[:, u, o:o + 128], src[:, r, e, 2:W], False, last)
+        inc(ins, "vp%d" % i)
+
+    i0 = 0
+    if d != 0:
+        wait("p", "dgo", 2)
+        spread(0)
+        i0 = 1
+    wait("p", "dg", 12)
+    wait("p", "dg0", 2)
+    keysum(0, T.kp0, 0, "kp0")
+    spread(i0)
+    spread(i0 + 1)
+    wait("p", "dgr", 2 * len(rest))
+    for r in range(1, N):
+        keysum(r, T.kp1, r - 1, "kp1")
+    for i in range(i0 + 2, 5):
+        spread(i)
+    wait("p", "gf", 4)
+    wait("p", "gi", 4)
+    for k, (r, c0, c) in enumerate(PIECES):
+        bank, n = (T.rp0, T.rp1)[k % 2], c // 2
+        if k >= 2:
+            wait("p", "ev%d" % (k - 2), 1)
+        t = (TT * r + c0 + c) // R - 1
+        for i, s in enumerate((0, 2, 1, 3)):
+            wait("p", "ch%d" % s, 2 * t)
+            for part in range(2):
+                o, b = 7 - 2 * s - part, TT * r + c0 + part * n
+                ins = PE.matmul(bank[:, 0:n], T.fm[:, s, o:o + 128], got[s][:, b:b + n], i == 0 and part == 0, i == 3 and part == 1)
+        inc(ins, "rp%d" % k)
+
+    def offs(s, t):
+        c = 128 * (t // 8) + 32 * s + 4 * (t % 8)
+        return T.off[:, c:c + 4]
+
+    def scatter(q, s, t):
+        wait(q, "vc%d" % need[t], 1)
+        wait(q, "vc%d" % need[t + 1], 1)
+        wait(q, "ch%d" % s, 2 * t)
+        out, src = tab[s][:, 0:H].indirect(offs(s, t)), T.val[:, R * t + 1:R * t + R + 1]
+        inc(V.tensor_copy(out, src) if q == "v" else SC.activation(out, src, F.Silu), "ch%d" % s)
+
+    def gather(q, s, t):
+        if t >= 8:
+            wait(q, "k1", 7)
+        wait(q, "ch%d" % s, 2 * t - 1)
+        out, src = got[s][:, R * t:R * t + R], tab[s][:, 0:H].indirect(offs(s, t))
+        inc(V.tensor_copy(out, src) if q == "v" else SC.activation(out, src, F.Identity), "ch%d" % s)
+
+    def evac(k):
+        r, c0, c = PIECES[k]
+        wait("v", "eb", 2)
+        wait("v", "rp%d" % k, 1)
+        inc(V.tensor_scalar(T.outb[:, r, c0 // 2:(c0 + c) // 2], (T.rp0, T.rp1)[k % 2][:, 0:c // 2], T.eb[:, 0:1], None, A.add), "ev%d" % k)
+
+    def copy(i):
+        r, u0, u1 = items[i]
+        wait("s", "vp%d" % i, 1)
+        inc(SC.activation(T.val[:, TT * r + R * u0:TT * r + R * u1], vpb[i % 4][:, 0:R * (u1 - u0)], F.Identity), "vc%d" % i)
+
+    dr, kr = digits(rest, "dgr"), keys(1, N, T.kp1, "kp1", "k1")
+    extra = {(2, 0): dr, (2, 1): dr, (4, 0): kr, (4, 1): kr, (5, 0): kr, (5, 1): kr}
+    ev_at = {9: 0, 17: 1, 25: 2, 28: 3, 30: 4}
+    wait("v", "tv", 2)
+    wait("v", "k0", 7)
+    for t in range(32):
+        if t > 0:
+            gather("v", 0, t)
+            gather("v", 1, t)
+        if (t, 0) in extra:
+            next(extra[(t, 0)])
+        if t in ev_at:
+            evac(ev_at[t])
+        if t < 31:
+            scatter("v", 0, t)
+            scatter("v", 1, t)
+        if (t, 1) in extra:
+            next(extra[(t, 1)])
+    evac(5)
+
+    wait("s", "c32", 1)
+    for i in range(7):
+        inc(SC.activation(tab[2 + i // 4][:, 1024 * (i % 4):1024 * (i % 4 + 1)], T.c32[:, :], F.Silu), "ts")
+    for i in range(i0 + 1):
+        copy(i)
+    cp_at = {1: i0 + 1}
+    for n, i in enumerate(range(i0 + 2, 5)):
+        cp_at[5 + 4 * n] = i
+    wait("s", "ts", 7)
+    wait("s", "tg", 1)
+    wait("s", "k0", 7)
+    for t in range(32):
+        if t > 0:
+            gather("s", 2, t)
+            gather("s", 3, t)
+        if t in cp_at:
+            copy(cp_at[t])
+        if t < 31:
+            scatter("s", 2, t)
+            scatter("s", 3, t)
+
+    nth = {}
+    for k, (r, c0, c) in enumerate(PIECES):
+        i = nth.get(r, 0)
+        nth[r] = i + 1
+        if r != d:
+            rid, pid, _ = topo.addr(T.cores[r])
+            m = topo.mask(core, T.cores[r])
+            wait("g", "ev%d" % k, 1)
+            g.remote_dma(T.land[:, d, c0 // 2:(c0 + c) // 2], T.outb[:, r, c0 // 2:(c0 + c) // 2],
+                         T.sem["res%d_%d" % (d, i)], T.sem.sent, pid, rid, m)
+            cnt["sent"] += len(topo.engines(core, T.cores[r]))
+            continue
+        for w in [d] + others:
+            src = T.outb if w == d else T.land
+            for yz, out in enumerate((T.y, T.z)):
+                q = "s" if (k == len(PIECES) - 1 and yz == 1) else "y"
+                if w == d:
+                    wait(q, "ev%d" % k, 1)
+                else:
+                    wait(q, "res%d_%d" % (w, i), len(topo.engines(T.cores[w], core)))
+                for e in range(2):
+                    p0 = 64 * yz + 32 * e
+                    inc(Q[q].dma_start(out[2 * w + e::8, c0:c0 + c], src[p0:p0 + 32, w, c0 // 2:(c0 + c) // 2]),
+                        "sta" if q == "y" else "stb", 16)
+    wait("g", "sent", cnt["sent"])
+    wait("y", "sta", cnt["sta"])
+    if "stb" in cnt:
+        wait("s", "stb", cnt["stb"])
+    for name in cnt:
+        if top.get(name, 0) < cnt[name]:
+            wait("p", name, cnt[name])

@@ -3,17 +3,20 @@ from concourse.mybir import AluOpType, ActivationFunctionType
 
 N, TT, R, H, S = 4, 512, 64, 4096, 8
 W = R + 2
-EW, FW = 145, 135
+EW, FW = 145, 198
+K = 1024
 EMPTY = 32.0
-PIECES = [(0, 0, 512), (1, 0, 512), (2, 0, 512), (3, 0, 256), (3, 256, 128), (3, 384, 128)]
+PIECES = [(0, 0, 512), (1, 0, 512), (2, 0, 512)] + [(3, c, 128) for c in range(0, TT, 128)]
 
 SCRATCH = {
-    "xq": ("sbuf", [128, 8, W], "int32"),
-    "xr": ("sbuf", [128, N, 2, W], "int32"),
-    "hq": ("sbuf", [128, 16], "int32"),
+    "xq": ("sbuf", [128, 2, N, W], "int32"),
+    "xu": ("sbuf", [128, N, 2, W], "uint16"),
+    "xf": ("sbuf", [128, 2, W], "float32"),
+    "hs": ("sbuf", [128, N, 2, 2, W], "bfloat16"),
+    "hl": ("sbuf", [128, N, 2, 2, W], "bfloat16"),
+    "h0": ("sbuf", [128, 2, 2, W], "bfloat16"),
+    "hq": ("sbuf", [128, 2, N, 2], "int32"),
     "hf": ("sbuf", [128, 8], "float32"),
-    "hb": ("sbuf", [128, N, 2, W], "bfloat16"),
-    "lb": ("sbuf", [128, N, 2, W], "bfloat16"),
     "dk": ("sbuf", [128, 128], "bfloat16"),
     "dg": ("sbuf", [128, 8, 128], "float16"),
     "d0": ("sbuf", [128, 4, 128], "float16"),
@@ -21,7 +24,6 @@ SCRATCH = {
     "fm": ("sbuf", [128, 4, FW], "bfloat16"),
     "cm": ("sbuf", [128, N, 128], "bfloat16"),
     "ct": ("sbuf", [128, TT], "bfloat16"),
-    "c32": ("sbuf", [128, 1024], "bfloat16"),
     "eb": ("sbuf", [128, 1], "float32"),
     "kt": ("sbuf", [128, TT], "float32"),
     "ki": ("sbuf", [128, TT], "int32"),
@@ -32,10 +34,7 @@ SCRATCH = {
     "tab1": ("sbuf", [128, H], "bfloat16"),
     "tab2": ("sbuf", [128, H], "float32"),
     "tab3": ("sbuf", [128, H], "float32"),
-    "got0": ("sbuf", [128, N * TT], "bfloat16"),
-    "got1": ("sbuf", [128, N * TT], "bfloat16"),
-    "got2": ("sbuf", [128, N * TT], "bfloat16"),
-    "got3": ("sbuf", [128, N * TT], "bfloat16"),
+    "got": ("sbuf", [128, 4, N * TT], "bfloat16"),
     "outb": ("sbuf", [128, N, 256], "float32"),
     "land": ("sbuf", [128, N, 256], "float32"),
     "kp0": ("psum", [128, 4, 4, 2, 16], "float32"),
@@ -47,12 +46,13 @@ SCRATCH = {
     "rp0": ("psum", [128, 512], "float32"),
     "rp1": ("psum", [128, 512], "float32"),
 }
-SEMAPHORES = (["ld", "ldh", "cz", "c32", "gk", "ge", "gf", "gct", "cs_z", "cs_m", "tv", "ts", "tg", "hf", "dz", "dg",
-               "gi", "eb", "dgo", "dg0", "dgr", "kp0", "kp1", "k0", "k1", "sent", "sta", "stb"]
+SEMAPHORES = (["ld", "ldh", "cz", "fz", "c32", "gk", "ge", "gf", "gct", "cs_z", "cs_m", "tv", "ts", "ts0", "tg", "df",
+               "hf", "dz", "dg", "gi", "eb", "dig", "digo", "dig0", "pk", "kp0", "kp1", "kp2", "k0", "k1", "k2",
+               "sent", "sta", "stb"]
               + ["ch%d" % i for i in range(4)] + ["arr%d" % i for i in range(N)]
               + ["vp%d" % i for i in range(5)] + ["vc%d" % i for i in range(5)]
-              + ["rp%d" % i for i in range(6)] + ["ev%d" % i for i in range(6)]
-              + ["res%d_%d" % (d, i) for d in range(N) for i in range(3)])
+              + ["rp%d" % i for i in range(7)] + ["ev%d" % i for i in range(7)]
+              + ["res%d" % i for i in range(4)])
 
 
 def rank_program(g, core, T, topo):
@@ -74,71 +74,111 @@ def rank_program(g, core, T, topo):
             seen[(q, name)] = n
             top[name] = max(top.get(name, 0), n)
 
+    def fill(out, n, value, name):
+        inc(g.iota(out, [[0, n]], value, 0, allow_small_or_imprecise_dtypes=True), name)
+
     tab = [T.tab0, T.tab1, T.tab2, T.tab3]
-    got = [T.got0, T.got1, T.got2, T.got3]
     vpb = [T.vp0, T.vp1, T.vp2, T.vp3]
     others = [r for r in range(N) if r != d]
+    spans = [(a, b) for a, b in ((0, d), (d + 1, N)) if a < b]
+    ND = 4 * len(spans)
 
-    def split(src, dst_ranks):
-        e = topo.engines(T.cores[src], T.cores[dst_ranks[0]])
+    def calls(src):
+        to = [r for r in range(N) if r != src]
+        e = topo.engines(T.cores[src], T.cores[to[0]])
         ev, od = e[0::2], e[1::2]
-        sets = [ev[:len(ev) // 2], ev[len(ev) // 2:], od]
-        return {r: sets[i] for i, r in enumerate(dst_ranks)}
+        if src < 2:
+            return [list(zip(to, [ev[:len(ev) // 2], ev[len(ev) // 2:], od]))]
+        return [[(0, e)], list(zip(to[1:], [ev, od]))]
 
-    def bits(es):
-        return sum(1 << e for e in es)
+    def send(call):
+        tr = []
+        for r, es in call:
+            rid, pid, _ = topo.addr(T.cores[r])
+            src, dst = (T.xu[:, r, :, :], T.xu[:, 0, :, :]) if d == 0 else (T.hs[:, r, :, :, :], T.hl[:, d, :, :, :])
+            tr.append(RemoteDMATransfer(dst_ids=[DstId(rid=rid, pnc=pid)], dma_engine_mask=sum(1 << e for e in es),
+                                        remote_sem=T.sem["arr%d" % d], src=src, dst=dst))
+            cnt["sent"] = cnt.get("sent", 0) + len(es)
+        g.remote_dma_fused(tr, local_sem=T.sem.sent)
 
-    for u in range(8):
-        q = SY if u % 2 == 0 else SC
-        if u == 0:
-            inc(q.dma_start(T.xq[0::8, :, 2:W], T.x[:, 0:R]), "ld", 16)
+    arr = {r: [len(es) for call in calls(r) for w, es in call if w == d][0] for r in others}
+
+    def have(q, r):
+        if r == 0:
+            wait(q, "dig0", 2 if d == 0 else 3)
+        elif r == d:
+            wait(q, "digo", 2)
         else:
-            inc(q.dma_start(T.xq[u::8, :, :], T.x[:, R * u - 2:R * u + R]), "ld", 16)
-    inc(SY.dma_start(T.xq[0::8, :, 0:2], T.x[:, TT - 2:TT]), "ld", 16)
+            wait(q, "arr%d" % r, arr[r])
+
+    def dig(r, j, e, c0, c1):
+        if r == 0:
+            return T.h0[:, j, e, c0:c1]
+        return (T.hs if r == d else T.hl)[:, r, j, e, c0:c1]
+
     for u in range(8):
-        inc(SY.dma_start(T.hq[u::8, :], T.hc[:, :]), "ldh", 16)
+        q = SC if u % 2 else SY
+        if u == 0:
+            inc(q.dma_start(T.xq[0::8, :, :, 2:W], T.x[:, 0:R]), "ld", 16)
+        else:
+            inc(q.dma_start(T.xq[u::8, :, :, :], T.x[:, R * u - 2:R * u + R]), "ld", 16)
+    inc(SY.dma_start(T.xq[0::8, :, :, 0:2], T.x[:, TT - 2:TT]), "ld", 16)
+    for u in range(8):
+        inc(SY.dma_start(T.hq[u::8, :, :, :], T.hc[:, :]), "ldh", 16)
     LD, LDH = cnt["ld"], cnt["ldh"]
 
     inc(g.iota(T.ct[32:64, :], [[1, 8], [0, R]], int(EMPTY), 0, allow_small_or_imprecise_dtypes=True), "gct")
     inc(g.iota(T.ct[0:32, :], [[0, 8], [1, R]], int(EMPTY), 0, allow_small_or_imprecise_dtypes=True), "gct")
     wait("g", "gct", 2)
     inc(g.iota(T.dk[:, :], [[1, 128]], 0, -1, allow_small_or_imprecise_dtypes=True), "gk")
-    wait("g", "cz", 2)
+    mine = calls(d)
+    if d == 0:
+        wait("g", "pk", 2)
+        send(mine[0])
+    wait("g", "cz", 1)
     for a in range(4):
         v = T.em[:, :, 17 + 32 * a:17 + 32 * a + 13:4]
         inc(g.affine_select(v, v, [[-1, 8], [-8, 4]], A.not_equal, 1.0, -32 * a, 1), "ge")
-    wait("g", "ld", LD)
-    masks = split(d, others)
-    tr = []
-    for r in others:
-        rid, pid, _ = topo.addr(T.cores[r])
-        tr.append(RemoteDMATransfer(dst_ids=[DstId(rid=rid, pnc=pid)], dma_engine_mask=bits(masks[r]),
-                                    remote_sem=T.sem["arr%d" % d], src=T.xq[:, 2 * r:2 * r + 2, :], dst=T.xr[:, d, :, :]))
-        cnt["sent"] = cnt.get("sent", 0) + len(masks[r])
-    g.remote_dma_fused(tr, local_sem=T.sem.sent)
-    arr = {r: len(split(r, [o for o in range(N) if o != r])[d]) for r in others}
-    inc(g.iota(T.tab3[:, 3072:4096], [[0, 1024]], int(EMPTY), 0, allow_small_or_imprecise_dtypes=True), "tg")
-    fy, fz = T.fm[:, :, 7:64:8], T.fm[:, :, 71:128:8]
-    inc(g.affine_select(fy, fy, [[0, 4], [-16, 2], [-32, 4]], A.not_equal, 64.0, -2, 1), "gf")
-    inc(g.affine_select(fz, fz, [[-4, 4], [-16, 2], [-32, 4]], A.not_equal, 1.0, 0, 1), "gf")
-    wait("g", "gf", 2)
-    inc(g.affine_select(fy, fy, [[0, 4], [-16, 2], [-32, 4]], A.not_equal, 1.0, -3, 1), "gf")
-    inc(g.affine_select(fz, fz, [[-4, 4], [-16, 2], [-32, 4]], A.not_equal, -1.0, -1, 1), "gf")
+    if d == 0:
+        fill(T.tab3[:, 2 * K + 512:H], 2 * K - 512, int(EMPTY), "tg")
+    else:
+        fill(T.tab3[:, 2 * K:2 * K + 512], 512, int(EMPTY), "tg")
+        wait("g", "dig", ND)
+        send(mine[0])
+        fill(T.tab3[:, 2 * K + 512:H], 2 * K - 512, int(EMPTY), "tg")
+    TG = cnt["tg"]
+    first_sent = cnt["sent"]
+    if len(mine) > 1:
+        wait("g", "arr0", arr[0])
+        send(mine[1])
+    fill(T.fm[:, :, :], 4 * FW, 0, "fz")
+    fill(T.got[:, :, 0:R], 4 * R, int(EMPTY), "gi")
+    fill(T.eb[:, :], 1, -1, "eb")
+    wait("g", "fz", 1)
+    for step in range(2):
+        wait("g", "gf", 4 * step)
+        for e in range(2):
+            fy, fz = T.fm[:, :, 70 + e:102:8], T.fm[:, :, 102 + e:134:8]
+            inc(g.affine_select(fy, fy, [[0, 4], [-32, 4]], A.not_equal, (64.0, 1.0)[step], -16 * e - 2 - step, 1), "gf")
+            inc(g.affine_select(fz, fz, [[-4, 4], [-32, 4]], A.not_equal, (1.0, -1.0)[step], -16 * e - step, 1), "gf")
+    wait("g", "gf", 8)
+    wait("g", "eb", 1)
+    for p0 in (64, 0):
+        fill(T.eb[p0:p0 + 32, :], 1, -(65 * int(EMPTY) + 1), "eb")
 
-    def digits(rs, name):
-        for r in rs:
-            if r == d:
-                wait("v", "ld", LD)
-            else:
-                wait("v", "arr%d" % r, arr[r])
-            src = T.xq[:, 2 * d:2 * d + 2, :] if r == d else T.xr[:, r, :, :]
-            inc(V.tensor_scalar(T.hb[:, r, :, :], src, 64.0, None, A.add), name)
-        yield
-        wait("v", name, len(rs))
-        for r in rs:
-            src = T.xq[:, 2 * d:2 * d + 2, :] if r == d else T.xr[:, r, :, :]
-            inc(V.tensor_tensor(T.lb[:, r, :, :], T.hb[:, r, :, :], src, A.subtract), name)
-        yield
+    wait("y", "ts0", 1)
+    if d == 0:
+        wait("y", "sent", first_sent)
+        inc(SY.dma_start(T.tab2[:, K:2 * K], T.tab2[:, 0:K]), "df", 16)
+        by_scalar = [(2, 2 * K, K), (2, 3 * K, K), (3, 0, K), (3, K, K), (3, 2 * K, 512), (1, K, K)]
+    else:
+        wait("y", "c32", 1)
+        inc(SY.dma_start(T.tab2[:, K:2 * K], T.tab2[:, 0:K]), "df", 16)
+        inc(SY.dma_start(T.tab1[:, K:2 * K], T.tab0[:, 0:K]), "df", 16)
+        inc(SY.dma_start(T.tab1[:, 2 * K:3 * K], T.tab0[:, 0:K]), "df", 16)
+        inc(SY.dma_start(T.tab2[:, 2 * K:3 * K], T.tab2[:, 0:K]), "df", 16)
+        by_scalar = [(2, 3 * K, K), (3, 0, K), (3, K, K)]
+    DF = cnt["df"]
 
     def keys(r0, r1, kp, kpn, name):
         n, c0, c1 = r1 - r0, 128 * r0, 128 * r1
@@ -156,30 +196,44 @@ def rank_program(g, core, T, topo):
             inc(V.tensor_copy(T.off[:, c0 + c:c1:4], T.kj[:, r0:r1, c, :]), name)
         yield
 
-    inc(V.memset(T.c32[:, :], EMPTY), "c32")
+    inc(V.memset(T.tab0[:, 0:K], EMPTY), "c32")
     inc(V.memset(T.em[:, :, :], 0.0), "cz")
-    inc(V.memset(T.fm[:, :, :], 0.0), "cz")
     inc(V.memset(T.cm[:, :, :], 0.0), "cs_z")
     inc(V.memset(T.d0[:, :, :], 0.0), "dz")
-    inc(V.memset(T.tab0[:, :], EMPTY), "tv")
+    inc(V.memset(T.tab0[:, K:2 * K], EMPTY), "tv")
     wait("v", "cs_z", 1)
     inc(V.memset(T.cm[0:1, :, 3::16], 1.0), "cs_m")
     inc(V.memset(T.cm[32:33, :, 2::16], 1.0), "cs_m")
     inc(V.memset(T.cm[64:65, :, 1::4], -1.0), "cs_m")
     for r in range(1, N):
         inc(V.memset(T.cm[64:65, r, 2::16], 8.0 * r), "cs_m")
-    inc(V.memset(T.ct[64:65, :], 1.0), "cs_m")
-    CSM = cnt["cs_m"]
     if d != 0:
-        for _ in digits([d], "dgo"):
-            pass
+        inc(V.memset(T.ct[64:65, :], 1.0), "cs_m")
+    wait("v", "ld", LD)
+    if d == 0:
+        for e in range(2):
+            inc(V.tensor_copy(T.xu[:, 1:N, e, :], T.xq[:, e, 1:N, :]), "pk")
+        inc(V.tensor_scalar(T.h0[:, 0, :, :], T.xq[:, :, 0, :], 64.0, None, A.add), "dig0")
+        inc(V.memset(T.ct[64:65, :], 1.0), "cs_m")
+        wait("v", "dig0", 1)
+        inc(V.tensor_tensor(T.h0[:, 1, :, :], T.h0[:, 0, :, :], T.xq[:, :, 0, :], A.subtract), "dig0")
+    else:
+        inc(V.tensor_scalar(T.hs[:, d, 0, :, :], T.xq[:, :, d, :], 64.0, None, A.add), "digo")
+        for a, b in spans:
+            inc(V.tensor_scalar(T.hs[:, a:b, 0, 0, :], T.xq[:, 0, a:b, :], 64.0, None, A.add), "dig")
+        wait("v", "digo", 1)
+        inc(V.tensor_tensor(T.hs[:, d, 1, :, :], T.hs[:, d, 0, :, :], T.xq[:, :, d, :], A.subtract), "digo")
+        for a, b in spans:
+            inc(V.tensor_scalar(T.hs[:, a:b, 0, 1, :], T.xq[:, 1, a:b, :], 64.0, None, A.add), "dig")
+        wait("v", "dig", ND // 2)
+        for e in range(2):
+            for a, b in spans:
+                inc(V.tensor_tensor(T.hs[:, a:b, 1, e, :], T.hs[:, a:b, 0, e, :], T.xq[:, e, a:b, :], A.subtract), "dig")
+    CSM = cnt["cs_m"]
     wait("v", "ldh", LDH)
-    inc(V.tensor_copy(T.hf[:, 0:4], T.hq[:, 4 * d:4 * d + 4]), "hf")
-    inc(V.tensor_scalar(T.hf[:, 4:8], T.hq[:, 4 * d:4 * d + 4], -1.0, None, A.mult), "hf")
-    for s in range(4):
-        inc(V.memset(got[s][:, 0:R], EMPTY), "gi")
-    inc(V.memset(T.eb[0:64, :], -(65.0 * EMPTY + 1.0)), "eb")
-    inc(V.memset(T.eb[64:128, :], -1.0), "eb")
+    inc(V.tensor_copy(T.hf[:, 0:4], T.hq[:, :, d, :]), "hf")
+    inc(V.tensor_scalar(T.hf[:, 4:8], T.hq[:, :, d, :], -1.0, None, A.mult), "hf")
+    inc(V.memset(T.tab0[:, 2 * K:3 * K], EMPTY), "tv")
     wait("v", "hf", 2)
     wait("v", "gk", 1)
     wait("v", "dz", 1)
@@ -187,11 +241,22 @@ def rank_program(g, core, T, topo):
         inc(V.tensor_scalar(T.dg[:, i, :], T.dk[:, :], 0.0, T.hf[:, i:i + 1], A.is_equal, A.mult), "dg")
     for i in range(4):
         inc(V.tensor_scalar(T.d0[:, i, 0::8], T.dk[:, 0::8], 0.0, T.hf[:, 2 * i:2 * i + 1], A.is_equal, A.mult), "dg")
-    inc(V.memset(T.tab1[:, :], EMPTY), "tv")
-    for _ in digits([0], "dg0"):
-        pass
+    if d != 0:
+        inc(V.memset(T.tab0[:, 3 * K:H], EMPTY), "tv")
+        inc(V.memset(T.tab1[:, 0:K], EMPTY), "tv")
+        wait("v", "arr0", arr[0])
+        inc(V.tensor_scalar(T.h0[:, 0, :, :], T.xu[:, 0, :, :], 64.0, None, A.add), "dig0")
+        inc(V.tensor_copy(T.xf[:, :, :], T.xu[:, 0, :, :]), "dig0")
+        wait("v", "dig0", 2)
+        inc(V.tensor_tensor(T.h0[:, 1, :, :], T.h0[:, 0, :, :], T.xf[:, :, :], A.subtract), "dig0")
+    inc(V.memset(T.tab1[:, 3 * K:H], EMPTY), "tv")
     for _ in keys(0, 1, T.kp0, "kp0", "k0"):
         pass
+    if d == 0:
+        inc(V.memset(T.tab0[:, 3 * K:H], EMPTY), "tv")
+        inc(V.memset(T.tab1[:, 0:K], EMPTY), "tv")
+        inc(V.memset(T.tab1[:, 2 * K:3 * K], EMPTY), "tv")
+    TV = cnt["tv"]
     rest = [r for r in range(1, N) if r != d]
 
     items = ([(d, 0, 8)] if d != 0 else []) + [(0, 0, 3), (0, 3, 8)] + [(r, 0, 8) for r in rest]
@@ -201,16 +266,19 @@ def rank_program(g, core, T, topo):
             need[8 * r + u] = i
 
     def keysum(r, kp, slot, name):
+        have("p", r)
+        if r > 0:
+            have("p", r - 1)
         for e in range(2):
             out = kp[:, slot, :, e, :]
             one = kp[:, slot, 0, e, 0:1]
             pa, pb, na, nb = T.dg[:, 2 * e, :], T.dg[:, 2 * e + 1, :], T.dg[:, 4 + 2 * e, :], T.dg[:, 5 + 2 * e, :]
             p0, n0 = T.d0[:, e, :], T.d0[:, 2 + e, :]
-            ms = [(out, pb, T.hb[:, r, e, 2:W]), (out, pa, T.hb[:, r, e, 1:W - 1]),
-                  (out, nb, T.lb[:, r, e, 2:W]), (out, na, T.lb[:, r, e, 1:W - 1]),
-                  (one, n0, T.hb[:, r, e, 1:2]), (one, p0, T.lb[:, r, e, 1:2])]
+            ms = [(out, pb, dig(r, 0, e, 2, W)), (out, pa, dig(r, 0, e, 1, W - 1)),
+                  (out, nb, dig(r, 1, e, 2, W)), (out, na, dig(r, 1, e, 1, W - 1)),
+                  (one, n0, dig(r, 0, e, 1, 2)), (one, p0, dig(r, 1, e, 1, 2))]
             if r > 0:
-                ms += [(one, p0, T.hb[:, r - 1, e, 1:2]), (one, n0, T.lb[:, r - 1, e, 1:2])]
+                ms += [(one, p0, dig(r - 1, 0, e, 1, 2)), (one, n0, dig(r - 1, 1, e, 1, 2))]
             for i, (o, l, x) in enumerate(ms):
                 ins = PE.matmul(o, l, x, i == 0, i == len(ms) - 1)
             inc(ins, name)
@@ -223,42 +291,45 @@ def rank_program(g, core, T, topo):
         wait("p", "ge", 4)
         wait("p", "gct", 2)
         wait("p", "cs_m", CSM)
+        have("p", r)
         PE.matmul(bank[:, 0:R * (u1 - u0)], T.cm[0:65, r, :], T.ct[0:65, R * u0:R * u1], True, False)
         for u in range(u0, u1):
             for e in range(2):
-                for j, src in enumerate((T.hb, T.lb)):
+                for j in range(2):
                     o = 17 - 16 * e - j
                     last = u == u1 - 1 and e == 1 and j == 1
-                    ins = PE.matmul(bank[:, R * (u - u0):R * (u - u0 + 1)], T.em[:, u, o:o + 128], src[:, r, e, 2:W], False, last)
+                    ins = PE.matmul(bank[:, R * (u - u0):R * (u - u0 + 1)], T.em[:, u, o:o + 128], dig(r, j, e, 2, W), False, last)
         inc(ins, "vp%d" % i)
 
     i0 = 0
     if d != 0:
-        wait("p", "dgo", 2)
         spread(0)
         i0 = 1
     wait("p", "dg", 12)
-    wait("p", "dg0", 2)
     keysum(0, T.kp0, 0, "kp0")
     spread(i0)
     spread(i0 + 1)
-    wait("p", "dgr", 2 * len(rest))
-    for r in range(1, N):
-        keysum(r, T.kp1, r - 1, "kp1")
-    for i in range(i0 + 2, 5):
+    keysum(1, T.kp1, 0, "kp1")
+    later = list(range(i0 + 2, 5))
+    if d != 1:
+        spread(later.pop(0))
+    wait("p", "k0", 7)
+    keysum(2, T.kp0, 0, "kp2")
+    keysum(3, T.kp0, 1, "kp2")
+    for i in later:
         spread(i)
-    wait("p", "gf", 4)
-    wait("p", "gi", 4)
+    wait("p", "gf", 8)
+    wait("p", "gi", 1)
     for k, (r, c0, c) in enumerate(PIECES):
         bank, n = (T.rp0, T.rp1)[k % 2], c // 2
         if k >= 2:
             wait("p", "ev%d" % (k - 2), 1)
-        t = (TT * r + c0 + c) // R - 1
-        for i, s in enumerate((0, 2, 1, 3)):
-            wait("p", "ch%d" % s, 2 * t)
-            for part in range(2):
-                o, b = 7 - 2 * s - part, TT * r + c0 + part * n
-                ins = PE.matmul(bank[:, 0:n], T.fm[:, s, o:o + 128], got[s][:, b:b + n], i == 0 and part == 0, i == 3 and part == 1)
+        for part in range(2):
+            b = TT * r + c0 + part * n
+            for i, s in enumerate((0, 2, 1, 3)):
+                wait("p", "ch%d" % s, 2 * ((b + n) // R - 1))
+                o = 70 - 64 * part - 2 * s
+                ins = PE.matmul(bank[:, 0:n], T.fm[:, s, o:o + 128], T.got[:, s, b:b + n], i == 0 and part == 0, i == 3 and part == 1)
         inc(ins, "rp%d" % k)
 
     def offs(s, t):
@@ -275,27 +346,39 @@ def rank_program(g, core, T, topo):
     def gather(q, s, t):
         if t >= 8:
             wait(q, "k1", 7)
+        if t >= 16:
+            wait(q, "k2", 7)
         wait(q, "ch%d" % s, 2 * t - 1)
-        out, src = got[s][:, R * t:R * t + R], tab[s][:, 0:H].indirect(offs(s, t))
+        out, src = T.got[:, s, R * t:R * t + R], tab[s][:, 0:H].indirect(offs(s, t))
         inc(V.tensor_copy(out, src) if q == "v" else SC.activation(out, src, F.Identity), "ch%d" % s)
 
     def evac(k):
         r, c0, c = PIECES[k]
-        wait("v", "eb", 2)
+        wait("v", "eb", 3)
         wait("v", "rp%d" % k, 1)
-        inc(V.tensor_scalar(T.outb[:, r, c0 // 2:(c0 + c) // 2], (T.rp0, T.rp1)[k % 2][:, 0:c // 2], T.eb[:, 0:1], None, A.add), "ev%d" % k)
+        out = (T.land if r == d else T.outb)[:, r, c0 // 2:(c0 + c) // 2]
+        inc(V.tensor_scalar(out, (T.rp0, T.rp1)[k % 2][:, 0:c // 2], T.eb[:, 0:1], None, A.add), "ev%d" % k)
 
-    def copy(i):
+    def copy(q, i):
         r, u0, u1 = items[i]
-        wait("s", "vp%d" % i, 1)
-        inc(SC.activation(T.val[:, TT * r + R * u0:TT * r + R * u1], vpb[i % 4][:, 0:R * (u1 - u0)], F.Identity), "vc%d" % i)
+        wait(q, "vp%d" % i, 1)
+        out, src = T.val[:, TT * r + R * u0:TT * r + R * u1], vpb[i % 4][:, 0:R * (u1 - u0)]
+        inc(V.tensor_copy(out, src) if q == "v" else SC.activation(out, src, F.Identity), "vc%d" % i)
 
-    dr, kr = digits(rest, "dgr"), keys(1, N, T.kp1, "kp1", "k1")
-    extra = {(2, 0): dr, (2, 1): dr, (4, 0): kr, (4, 1): kr, (5, 0): kr, (5, 1): kr}
-    ev_at = {9: 0, 17: 1, 25: 2, 28: 3, 30: 4}
-    wait("v", "tv", 2)
+    k1, k2 = keys(1, 2, T.kp1, "kp1", "k1"), keys(2, N, T.kp0, "kp2", "k2")
+    extra = {(5, 0): k1, (5, 1): k1, (6, 0): k1, (6, 1): k1, (12, 0): k2, (12, 1): k2, (13, 0): k2, (13, 1): k2}
+    ev_at = {14: 0, 17: 1, 25: 2, 26: 3, 28: 4, 30: 5}
+    NS = len(by_scalar)
+    wait("v", "tv", TV)
+    wait("v", "c32", 1)
+    wait("v", "ts0", 1)
+    wait("v", "ts", NS)
+    if d != 0:
+        wait("v", "df", DF)
     wait("v", "k0", 7)
     for t in range(32):
+        if t == 8 * items[4][0] - 1:
+            copy("v", 4)
         if t > 0:
             gather("v", 0, t)
             gather("v", 1, t)
@@ -308,53 +391,51 @@ def rank_program(g, core, T, topo):
             scatter("v", 1, t)
         if (t, 1) in extra:
             next(extra[(t, 1)])
-    evac(5)
+    evac(6)
 
     wait("s", "c32", 1)
-    for i in range(7):
-        inc(SC.activation(tab[2 + i // 4][:, 1024 * (i % 4):1024 * (i % 4 + 1)], T.c32[:, :], F.Silu), "ts")
+    inc(SC.activation(T.tab2[:, 0:K], T.tab0[:, 0:K], F.Silu), "ts0")
+    for s, c0, n in by_scalar:
+        inc(SC.activation(tab[s][:, c0:c0 + n], T.tab0[:, 0:n], F.Identity), "ts")
     for i in range(i0 + 1):
-        copy(i)
-    cp_at = {1: i0 + 1}
-    for n, i in enumerate(range(i0 + 2, 5)):
-        cp_at[5 + 4 * n] = i
-    wait("s", "ts", 7)
-    wait("s", "tg", 1)
+        copy("s", i)
+    cp_at = {2: i0 + 1}
+    for i in range(i0 + 2, 4):
+        cp_at[8 * items[i][0] - 1] = i
+    wait("s", "ts0", 1)
+    wait("s", "ts", NS)
+    wait("s", "tg", TG)
+    wait("s", "df", DF)
     wait("s", "k0", 7)
     for t in range(32):
+        if t in cp_at:
+            copy("s", cp_at[t])
         if t > 0:
             gather("s", 2, t)
             gather("s", 3, t)
-        if t in cp_at:
-            copy(cp_at[t])
         if t < 31:
             scatter("s", 2, t)
             scatter("s", 3, t)
 
     nth = {}
     for k, (r, c0, c) in enumerate(PIECES):
-        i = nth.get(r, 0)
+        i, n = nth.get(r, 0), c // 2
         nth[r] = i + 1
         if r != d:
             rid, pid, _ = topo.addr(T.cores[r])
-            m = topo.mask(core, T.cores[r])
             wait("g", "ev%d" % k, 1)
-            g.remote_dma(T.land[:, d, c0 // 2:(c0 + c) // 2], T.outb[:, r, c0 // 2:(c0 + c) // 2],
-                         T.sem["res%d_%d" % (d, i)], T.sem.sent, pid, rid, m)
+            g.remote_dma(T.land[:, d, c0 // 2:c0 // 2 + n], T.outb[:, r, c0 // 2:c0 // 2 + n],
+                         T.sem["res%d" % i], T.sem.sent, pid, rid, topo.mask(core, T.cores[r]))
             cnt["sent"] += len(topo.engines(core, T.cores[r]))
             continue
-        for w in [d] + others:
-            src = T.outb if w == d else T.land
-            for yz, out in enumerate((T.y, T.z)):
-                q = "s" if (k == len(PIECES) - 1 and yz == 1) else "y"
-                if w == d:
-                    wait(q, "ev%d" % k, 1)
-                else:
-                    wait(q, "res%d_%d" % (w, i), len(topo.engines(T.cores[w], core)))
-                for e in range(2):
-                    p0 = 64 * yz + 32 * e
-                    inc(Q[q].dma_start(out[2 * w + e::8, c0:c0 + c], src[p0:p0 + 32, w, c0 // 2:(c0 + c) // 2]),
-                        "sta" if q == "y" else "stb", 16)
+        for yz, out in enumerate((T.y, T.z)):
+            q = "s" if (k == len(PIECES) - 1 and yz == 1) else "y"
+            wait(q, "ev%d" % k, 1)
+            wait(q, "res%d" % i, sum(len(topo.engines(T.cores[w], core)) for w in others))
+            for part in range(2):
+                p0 = 64 * part + 32 * yz
+                inc(Q[q].dma_start(out[:, c0 + part * n:c0 + part * n + n], T.land[p0:p0 + 32, :, c0 // 2:c0 // 2 + n]),
+                    "sta" if q == "y" else "stb", 16)
     wait("g", "sent", cnt["sent"])
     wait("y", "sta", cnt["sta"])
     if "stb" in cnt:

@@ -2,25 +2,30 @@ from concourse.bass import DstId, RemoteDMATransfer
 from concourse.mybir import AluOpType, ActivationFunctionType
 
 N, TT, R, H, S = 4, 512, 64, 4096, 8
-W = R + 2
-EW, FW = 145, 198
+NR = N * TT // R
+QW = 128
+Z = 8
+W = Z + QW
+EW, DW, FW, FZ = 130, 136, 136, 7
 K = 1024
-EMPTY = 32.0
-PIECES = [(0, 0, 512), (1, 0, 512), (2, 0, 512)] + [(3, c, 128) for c in range(0, TT, 128)]
+EMPTY, LIFT = 48, 32
+CQ = 2
+PIECES = [(0, 8), (8, 8), (16, 8), (24, 2), (26, 2), (28, 2), (30, 1), (31, 1)]
 
 SCRATCH = {
-    "xq": ("sbuf", [128, 2, N, W], "int32"),
-    "xu": ("sbuf", [128, N, 2, W], "uint16"),
-    "xf": ("sbuf", [128, 2, W], "float32"),
-    "hs": ("sbuf", [128, N, 2, 2, W], "bfloat16"),
-    "hl": ("sbuf", [128, N, 2, 2, W], "bfloat16"),
-    "h0": ("sbuf", [128, 2, 2, W], "bfloat16"),
-    "hq": ("sbuf", [128, 2, N, 2], "int32"),
-    "hf": ("sbuf", [128, 8], "float32"),
-    "dk": ("sbuf", [128, 128], "bfloat16"),
-    "dg": ("sbuf", [128, 8, 128], "float16"),
-    "d0": ("sbuf", [128, 4, 128], "float16"),
-    "em": ("sbuf", [128, 8, EW], "bfloat16"),
+    "xq": ("sbuf", [128, N, QW], "int32"),
+    "xu": ("sbuf", [128, N, QW], "uint16"),
+    "xl": ("sbuf", [128, N, QW], "uint16"),
+    "xf": ("sbuf", [128, N, QW], "float32"),
+    "hs": ("sbuf", [128, N, 2, W], "bfloat16"),
+    "hd": ("sbuf", [128, N, 2, W], "bfloat16"),
+    "ds": ("sbuf", [128, 2, DW], "float16"),
+    "dw": ("sbuf", [128, 2, DW], "float16"),
+    "hq": ("sbuf", [128, 2], "int32"),
+    "hf": ("sbuf", [128, 2], "float32"),
+    "dk": ("sbuf", [128, DW], "bfloat16"),
+    "dg": ("sbuf", [128, 4, DW], "float16"),
+    "em": ("sbuf", [128, 4, EW], "bfloat16"),
     "fm": ("sbuf", [128, 4, FW], "bfloat16"),
     "cm": ("sbuf", [128, N, 128], "bfloat16"),
     "ct": ("sbuf", [128, TT], "bfloat16"),
@@ -30,13 +35,16 @@ SCRATCH = {
     "kj": ("sbuf", [128, N, 4, 32], "int32"),
     "off": ("sbuf", [128, TT], "uint16"),
     "val": ("sbuf", [128, N * TT], "float32"),
-    "tab0": ("sbuf", [128, H], "bfloat16"),
-    "tab1": ("sbuf", [128, H], "bfloat16"),
-    "tab2": ("sbuf", [128, H], "float32"),
-    "tab3": ("sbuf", [128, H], "float32"),
+    "tabv": ("sbuf", [128, 2 * H], "bfloat16"),
+    "tabs": ("sbuf", [128, 2 * H], "float32"),
     "got": ("sbuf", [128, 4, N * TT], "bfloat16"),
     "outb": ("sbuf", [128, N, 256], "float32"),
-    "land": ("sbuf", [128, N, 256], "float32"),
+    "land0": ("dram", [N, 128, 256], "float32"),
+    "land1": ("dram", [N, 128, 64], "float32"),
+    "land2": ("dram", [N, 128, 64], "float32"),
+    "land3": ("dram", [N, 128, 64], "float32"),
+    "land4": ("dram", [N, 128, 32], "float32"),
+    "land5": ("dram", [N, 128, 32], "float32"),
     "kp0": ("psum", [128, 4, 4, 2, 16], "float32"),
     "kp1": ("psum", [128, 4, 4, 2, 16], "float32"),
     "vp0": ("psum", [128, 512], "float32"),
@@ -46,13 +54,13 @@ SCRATCH = {
     "rp0": ("psum", [128, 512], "float32"),
     "rp1": ("psum", [128, 512], "float32"),
 }
-SEMAPHORES = (["ld", "ldh", "cz", "fz", "c32", "gk", "ge", "gf", "gct", "cs_z", "cs_m", "tv", "ts", "ts0", "tg", "df",
-               "hf", "dz", "dg", "gi", "eb", "dig", "digo", "dig0", "pk", "kp0", "kp1", "kp2", "k0", "k1", "k2",
-               "sent", "sta", "stb"]
+SEMAPHORES = (["tw", "dfv", "ld0", "ld1", "ld2", "ld3", "ds", "dz", "ldh", "cz", "fz", "c32", "xz", "kz", "gk", "ge", "gf", "gct", "cs_z", "cs_m", "tv", "ts", "ts0", "tg",
+               "df", "hf", "dg", "gi", "eb", "dig0", "dig1", "dig2", "dig3", "pk", "sent", "sta", "stb"]
+              + ["kp%d" % i for i in range(N)] + ["k%d" % i for i in range(N)] + ["ko%d" % i for i in range(3)]
               + ["ch%d" % i for i in range(4)] + ["arr%d" % i for i in range(N)]
               + ["vp%d" % i for i in range(5)] + ["vc%d" % i for i in range(5)]
-              + ["rp%d" % i for i in range(7)] + ["ev%d" % i for i in range(7)]
-              + ["res%d" % i for i in range(4)])
+              + ["rp%d" % i for i in range(len(PIECES))] + ["ev%d" % i for i in range(len(PIECES))]
+              + ["res%d" % i for i in range(5)])
 
 
 def rank_program(g, core, T, topo):
@@ -74,368 +82,390 @@ def rank_program(g, core, T, topo):
             seen[(q, name)] = n
             top[name] = max(top.get(name, 0), n)
 
+    def iota(out, pattern, base, step, name):
+        inc(g.iota(out, pattern, base, step, allow_small_or_imprecise_dtypes=True), name)
+
     def fill(out, n, value, name):
-        inc(g.iota(out, [[0, n]], value, 0, allow_small_or_imprecise_dtypes=True), name)
+        iota(out, [[0, n]], value, 0, name)
 
-    tab = [T.tab0, T.tab1, T.tab2, T.tab3]
-    vpb = [T.vp0, T.vp1, T.vp2, T.vp3]
     others = [r for r in range(N) if r != d]
-    spans = [(a, b) for a, b in ((0, d), (d + 1, N)) if a < b]
-    ND = 4 * len(spans)
+    early = d < 2
+    order = others if d != 1 else [0, 3, 2]
 
-    def calls(src):
-        to = [r for r in range(N) if r != src]
-        e = topo.engines(T.cores[src], T.cores[to[0]])
-        ev, od = e[0::2], e[1::2]
-        if src < 2:
-            return [list(zip(to, [ev[:len(ev) // 2], ev[len(ev) // 2:], od]))]
-        return [[(0, e)], list(zip(to[1:], [ev, od]))]
+    def send(r, src, dst, sem):
+        rid, pid, _ = topo.addr(T.cores[r])
+        g.remote_dma(dst, src, T.sem[sem], T.sem.sent, pid, rid, topo.mask(core, T.cores[r]))
+        cnt["sent"] = cnt.get("sent", 0) + len(topo.engines(core, T.cores[r]))
 
-    def send(call):
-        tr = []
-        for r, es in call:
-            rid, pid, _ = topo.addr(T.cores[r])
-            src, dst = (T.xu[:, r, :, :], T.xu[:, 0, :, :]) if d == 0 else (T.hs[:, r, :, :, :], T.hl[:, d, :, :, :])
-            tr.append(RemoteDMATransfer(dst_ids=[DstId(rid=rid, pnc=pid)], dma_engine_mask=sum(1 << e for e in es),
-                                        remote_sem=T.sem["arr%d" % d], src=src, dst=dst))
-            cnt["sent"] = cnt.get("sent", 0) + len(es)
-        g.remote_dma_fused(tr, local_sem=T.sem.sent)
+    def deal():
+        for i, r in enumerate(order):
+            wait("g", "pk", i + 1)
+            if early:
+                send(r, T.xu[:, r, :], T.xl[:, d, :], "arr%d" % d)
+            else:
+                send(r, T.hs[:, r, :, :], T.hd[:, d, :, :], "arr%d" % d)
 
-    arr = {r: [len(es) for call in calls(r) for w, es in call if w == d][0] for r in others}
+    arr = {r: len(topo.engines(T.cores[r], core)) for r in others}
 
-    def have(q, r):
-        if r == 0:
-            wait(q, "dig0", 2 if d == 0 else 3)
-        elif r == d:
-            wait(q, "digo", 2)
-        else:
+    def have(q, r, j=1):
+        if r > 1 and r != d:
             wait(q, "arr%d" % r, arr[r])
-
-    def dig(r, j, e, c0, c1):
-        if r == 0:
-            return T.h0[:, j, e, c0:c1]
-        return (T.hs if r == d else T.hl)[:, r, j, e, c0:c1]
-
-    for u in range(8):
-        q = SC if u % 2 else SY
-        if u == 0:
-            inc(q.dma_start(T.xq[0::8, :, :, 2:W], T.x[:, 0:R]), "ld", 16)
         else:
-            inc(q.dma_start(T.xq[u::8, :, :, :], T.x[:, R * u - 2:R * u + R]), "ld", 16)
-    inc(SY.dma_start(T.xq[0::8, :, :, 0:2], T.x[:, TT - 2:TT]), "ld", 16)
-    for u in range(8):
-        inc(SY.dma_start(T.hq[u::8, :, :, :], T.hc[:, :]), "ldh", 16)
-    LD, LDH = cnt["ld"], cnt["ldh"]
+            wait(q, "dig%d" % r, 1 if j == 0 else 2 if r == d else 3)
 
-    inc(g.iota(T.ct[32:64, :], [[1, 8], [0, R]], int(EMPTY), 0, allow_small_or_imprecise_dtypes=True), "gct")
-    inc(g.iota(T.ct[0:32, :], [[0, 8], [1, R]], int(EMPTY), 0, allow_small_or_imprecise_dtypes=True), "gct")
-    wait("g", "gct", 2)
-    inc(g.iota(T.dk[:, :], [[1, 128]], 0, -1, allow_small_or_imprecise_dtypes=True), "gk")
-    mine = calls(d)
-    if d == 0:
-        wait("g", "pk", 2)
-        send(mine[0])
+    def dig(r, j, c0=0, c1=QW):
+        return (T.hs if r == d and not early else T.hd)[:, r, j, Z + c0:Z + c1]
+
+    for i, r in enumerate(order + [d] if early else [d] + order):
+        inc((SY, SC)[i % 2].dma_start(T.xq[:, r, :], T.x[32 * r:32 * r + 32, :]), "ld%d" % r, 16)
+    for q in range(4):
+        inc(SY.dma_start(T.hq[q::4, :], T.hc[32 * d:32 * d + 32, :]), "ldh", 16)
+    LDH = cnt["ldh"]
+
+    wait("g", "kz", 1)
+    iota(T.dk[:, 2:130:2], [[-32, 4], [-4, 4], [-1, 4]], 0, 1, "gk")
     wait("g", "cz", 1)
-    for a in range(4):
-        v = T.em[:, :, 17 + 32 * a:17 + 32 * a + 13:4]
-        inc(g.affine_select(v, v, [[-1, 8], [-8, 4]], A.not_equal, 1.0, -32 * a, 1), "ge")
-    if d == 0:
-        fill(T.tab3[:, 2 * K + 512:H], 2 * K - 512, int(EMPTY), "tg")
-    else:
-        fill(T.tab3[:, 2 * K:2 * K + 512], 512, int(EMPTY), "tg")
-        wait("g", "dig", ND)
-        send(mine[0])
-        fill(T.tab3[:, 2 * K + 512:H], 2 * K - 512, int(EMPTY), "tg")
+    v = T.em[:, :, 1:129:4]
+    inc(g.affine_select(v, v, [[-1, 4], [-4, 32]], A.not_equal, 1.0, 0, 1), "ge")
+    if early:
+        deal()
+    wait("g", "ge", 1)
+    for u0, u1 in ((0, 4), (4, 8)):
+        iota(T.ct[32:64, R * u0:R * u1], [[1, u1 - u0], [0, R]], EMPTY + u0, 0, "gct")
+        iota(T.ct[0:32, R * u0:R * u1], [[0, u1 - u0], [1, R]], EMPTY, 0, "gct")
+    wait("g", "gct", 3)
+    G0 = 7 * K + 512 if early else 6 * K
+    fill(T.tabs[:, G0:8 * K], 8 * K - G0, EMPTY, "tg")
     TG = cnt["tg"]
-    first_sent = cnt["sent"]
-    if len(mine) > 1:
+    if not early:
         wait("g", "arr0", arr[0])
-        send(mine[1])
+        deal()
+    first_sent = cnt["sent"]
     fill(T.fm[:, :, :], 4 * FW, 0, "fz")
-    fill(T.got[:, :, 0:R], 4 * R, int(EMPTY), "gi")
-    fill(T.eb[:, :], 1, -1, "eb")
+    fill(T.got[:, :, 0:R], 4 * R, EMPTY, "gi")
+    fill(T.eb[0:64, :], 1, -(65 * EMPTY + 1), "eb")
     wait("g", "fz", 1)
+    fy, fz = T.fm[:, :, FZ:FZ + 64:8], T.fm[:, :, FZ + 64:FZ + 128:8]
     for step in range(2):
-        wait("g", "gf", 4 * step)
-        for e in range(2):
-            fy, fz = T.fm[:, :, 70 + e:102:8], T.fm[:, :, 102 + e:134:8]
-            inc(g.affine_select(fy, fy, [[0, 4], [-32, 4]], A.not_equal, (64.0, 1.0)[step], -16 * e - 2 - step, 1), "gf")
-            inc(g.affine_select(fz, fz, [[-4, 4], [-32, 4]], A.not_equal, (1.0, -1.0)[step], -16 * e - step, 1), "gf")
-    wait("g", "gf", 8)
-    wait("g", "eb", 1)
-    for p0 in (64, 0):
-        fill(T.eb[p0:p0 + 32, :], 1, -(65 * int(EMPTY) + 1), "eb")
+        wait("g", "gf", 2 * step)
+        inc(g.affine_select(fy, fy, [[0, 4], [-16, 8]], A.not_equal, (64.0, 1.0)[step], -2 - step, 1), "gf")
+        inc(g.affine_select(fz, fz, [[-4, 4], [-16, 8]], A.not_equal, 1.0, -step, 1), "gf")
+    wait("g", "gf", 4)
+    fill(T.eb[64:128, :], 1, -(2 * EMPTY + 1), "eb")
 
-    wait("y", "ts0", 1)
-    if d == 0:
+    S1 = (6 * K + 512, 7 * K, 5 * K, 5 * K)[d]
+    by_scalar, by_dma = range(3 * K, S1, K), [1] if early else [1, 5]
+    wait("y", "c32", 2)
+    for i in (4, 5):
+        inc(SY.dma_start(T.tabv[:, i * K:(i + 1) * K], T.tabv[:, 0:K]), "dfv", 16)
+    if early:
         wait("y", "sent", first_sent)
-        inc(SY.dma_start(T.tab2[:, K:2 * K], T.tab2[:, 0:K]), "df", 16)
-        by_scalar = [(2, 2 * K, K), (2, 3 * K, K), (3, 0, K), (3, K, K), (3, 2 * K, 512), (1, K, K)]
-    else:
-        wait("y", "c32", 1)
-        inc(SY.dma_start(T.tab2[:, K:2 * K], T.tab2[:, 0:K]), "df", 16)
-        inc(SY.dma_start(T.tab1[:, K:2 * K], T.tab0[:, 0:K]), "df", 16)
-        inc(SY.dma_start(T.tab1[:, 2 * K:3 * K], T.tab0[:, 0:K]), "df", 16)
-        inc(SY.dma_start(T.tab2[:, 2 * K:3 * K], T.tab2[:, 0:K]), "df", 16)
-        by_scalar = [(2, 3 * K, K), (3, 0, K), (3, K, K)]
-    DF = cnt["df"]
+    wait("y", "ts0", 2)
+    for i in by_dma:
+        inc(SY.dma_start(T.tabs[:, i * K:(i + 1) * K], T.tabs[:, 0:K]), "df", 16)
+    DF = cnt.get("df", 0)
 
-    def keys(r0, r1, kp, kpn, name):
-        n, c0, c1 = r1 - r0, 128 * r0, 128 * r1
-        wait("v", kpn, 2 * n)
-        inc(V.transpose(T.kt[:, c0:c1], kp[:, 0:n, :, :, :]), name)
+    KP = [(T.kp0, 0), (T.kp1, 0), (T.kp0, 0), (T.kp1, 0)]
+
+    def keys(r):
+        kp, slot = KP[r]
+        c0, c1, name = 128 * r, 128 * r + 128, "k%d" % r
+        wait("v", "kp%d" % r, 1)
+        inc(V.transpose(T.kt[:, c0:c1], kp[:, slot, :, :, :]), name)
         yield
         wait("v", name, 1)
         inc(V.tensor_copy(T.ki[:, c0:c1], T.kt[:, c0:c1]), name)
         yield
         wait("v", name, 2)
-        inc(V.tensor_scalar(T.kj[:, r0:r1, :, :], T.ki[:, c0:c1], S, H - 1, A.logical_shift_right, A.bitwise_and), name)
-        yield
-        wait("v", name, 3)
-        for c in range(4):
-            inc(V.tensor_copy(T.off[:, c0 + c:c1:4], T.kj[:, r0:r1, c, :]), name)
+        inc(V.tensor_scalar(T.kj[:, r, :, :], T.ki[:, c0:c1], S, H - 1, A.logical_shift_right, A.bitwise_and), name)
         yield
 
-    inc(V.memset(T.tab0[:, 0:K], EMPTY), "c32")
+    def lists(r0, r1, name):
+        for c in range(4):
+            for r in range(r0, r1):
+                wait("v", "k%d" % r, 3)
+            inc(V.tensor_copy(T.off[:, 128 * r0 + c:128 * r1:4], T.kj[:, r0:r1, c, :]), name)
+            yield
+
+    def vfill(c0, c1, name="tv"):
+        inc(V.memset(T.tabv[:, c0:c1], float(EMPTY)), name)
+
+    def pack(i):
+        wait("v", "ld%d" % order[i], 16)
+        inc(V.tensor_copy(T.xu[:, order[i], :], T.xq[:, order[i], :]), "pk")
+
+    def digits(r):
+        if r != d:
+            name = "dig%d" % r
+            wait("v", "arr%d" % r, arr[r])
+            inc(V.tensor_scalar(dig(r, 0), T.xl[:, r, :], float(LIFT), None, A.add), name)
+            inc(V.tensor_copy(T.xf[:, r, :], T.xl[:, r, :]), name)
+            yield
+            wait("v", name, 2)
+            inc(V.tensor_tensor_scan(dig(r, 1), T.xf[:, r, :], dig(r, 0), 0.0, A.max, A.subtract), name)
+            yield
+
+    def low(r, name):
+        out = dig(d, 1) if r == d else T.hs[:, r, 1, Z:W]
+        inc(V.tensor_tensor(out, T.xq[:, r, :], dig(d, 0) if r == d else T.hs[:, r, 0, Z:W], A.subtract), name)
+
+    vfill(0, 256, "c32")
+    inc(V.memset(T.dk[:, :], 200.0), "kz")
     inc(V.memset(T.em[:, :, :], 0.0), "cz")
+    vfill(256, K, "c32")
+    inc(V.memset(T.hd[:, 0:2, :, 0:Z], 0.0), "xz")
+    if not early:
+        inc(V.memset(T.hs[:, :, :, 0:Z], 0.0), "xz")
     inc(V.memset(T.cm[:, :, :], 0.0), "cs_z")
-    inc(V.memset(T.d0[:, :, :], 0.0), "dz")
-    inc(V.memset(T.tab0[:, K:2 * K], EMPTY), "tv")
+    inc(V.memset(T.dw[:, :, :], 0.0), "dz")
+    if early:
+        pack(0)
     wait("v", "cs_z", 1)
     inc(V.memset(T.cm[0:1, :, 3::16], 1.0), "cs_m")
     inc(V.memset(T.cm[32:33, :, 2::16], 1.0), "cs_m")
-    inc(V.memset(T.cm[64:65, :, 1::4], -1.0), "cs_m")
+    inc(V.memset(T.cm[64:65, :, 1::4], 2.0 * EMPTY + 1), "cs_m")
+    if early:
+        pack(1)
     for r in range(1, N):
         inc(V.memset(T.cm[64:65, r, 2::16], 8.0 * r), "cs_m")
-    if d != 0:
-        inc(V.memset(T.ct[64:65, :], 1.0), "cs_m")
-    wait("v", "ld", LD)
-    if d == 0:
-        for e in range(2):
-            inc(V.tensor_copy(T.xu[:, 1:N, e, :], T.xq[:, e, 1:N, :]), "pk")
-        inc(V.tensor_scalar(T.h0[:, 0, :, :], T.xq[:, :, 0, :], 64.0, None, A.add), "dig0")
-        inc(V.memset(T.ct[64:65, :], 1.0), "cs_m")
-        wait("v", "dig0", 1)
-        inc(V.tensor_tensor(T.h0[:, 1, :, :], T.h0[:, 0, :, :], T.xq[:, :, 0, :], A.subtract), "dig0")
-    else:
-        inc(V.tensor_scalar(T.hs[:, d, 0, :, :], T.xq[:, :, d, :], 64.0, None, A.add), "digo")
-        for a, b in spans:
-            inc(V.tensor_scalar(T.hs[:, a:b, 0, 0, :], T.xq[:, 0, a:b, :], 64.0, None, A.add), "dig")
-        wait("v", "digo", 1)
-        inc(V.tensor_tensor(T.hs[:, d, 1, :, :], T.hs[:, d, 0, :, :], T.xq[:, :, d, :], A.subtract), "digo")
-        for a, b in spans:
-            inc(V.tensor_scalar(T.hs[:, a:b, 0, 1, :], T.xq[:, 1, a:b, :], 64.0, None, A.add), "dig")
-        wait("v", "dig", ND // 2)
-        for e in range(2):
-            for a, b in spans:
-                inc(V.tensor_tensor(T.hs[:, a:b, 1, e, :], T.hs[:, a:b, 0, e, :], T.xq[:, e, a:b, :], A.subtract), "dig")
+    if early:
+        pack(2)
+    inc(V.memset(T.ct[64:65, :], 1.0), "cs_m")
     CSM = cnt["cs_m"]
+    vfill(K, 2 * K)
+    if early:
+        wait("v", "ld%d" % d, 16)
+        inc(V.tensor_scalar(dig(d, 0), T.xq[:, d, :], float(LIFT), None, A.add), "dig%d" % d)
+    else:
+        for r in range(N):
+            wait("v", "ld%d" % r, 16)
+        inc(V.tensor_scalar(T.hs[:, :, 0, Z:W], T.xq[:, :, :], float(LIFT), None, A.add), "dig%d" % d)
+    vfill(2 * K, 3 * K)
+    wait("v", "dig%d" % d, 1)
+    low(d, "dig%d" % d)
     wait("v", "ldh", LDH)
-    inc(V.tensor_copy(T.hf[:, 0:4], T.hq[:, :, d, :]), "hf")
-    inc(V.tensor_scalar(T.hf[:, 4:8], T.hq[:, :, d, :], -1.0, None, A.mult), "hf")
-    inc(V.memset(T.tab0[:, 2 * K:3 * K], EMPTY), "tv")
-    wait("v", "hf", 2)
+    inc(V.tensor_copy(T.hf[:, :], T.hq[:, :]), "hf")
+    vfill(3 * K, 4 * K)
+    wait("v", "hf", 1)
     wait("v", "gk", 1)
     wait("v", "dz", 1)
-    for i in range(8):
-        inc(V.tensor_scalar(T.dg[:, i, :], T.dk[:, :], 0.0, T.hf[:, i:i + 1], A.is_equal, A.mult), "dg")
+    wait("v", "xz", cnt["xz"])
+    for e in range(2):
+        inc(V.tensor_scalar(T.ds[:, e, :], T.dk[:, :], 16.0 * e, T.hf[:, 0:1], A.is_equal, A.mult), "ds")
+        inc(V.tensor_scalar(T.dw[:, e, 8::8], T.dk[:, 8::8], 16.0 * e, T.hf[:, 0:1], A.is_equal, A.mult), "dg")
     for i in range(4):
-        inc(V.tensor_scalar(T.d0[:, i, 0::8], T.dk[:, 0::8], 0.0, T.hf[:, 2 * i:2 * i + 1], A.is_equal, A.mult), "dg")
-    if d != 0:
-        inc(V.memset(T.tab0[:, 3 * K:H], EMPTY), "tv")
-        inc(V.memset(T.tab1[:, 0:K], EMPTY), "tv")
-        wait("v", "arr0", arr[0])
-        inc(V.tensor_scalar(T.h0[:, 0, :, :], T.xu[:, 0, :, :], 64.0, None, A.add), "dig0")
-        inc(V.tensor_copy(T.xf[:, :, :], T.xu[:, 0, :, :]), "dig0")
-        wait("v", "dig0", 2)
-        inc(V.tensor_tensor(T.h0[:, 1, :, :], T.h0[:, 0, :, :], T.xf[:, :, :], A.subtract), "dig0")
-    inc(V.memset(T.tab1[:, 3 * K:H], EMPTY), "tv")
-    for _ in keys(0, 1, T.kp0, "kp0", "k0"):
+        inc(V.tensor_scalar(T.dg[:, i, :], T.dk[:, :], 16.0 * (i // 2), T.hf[:, i % 2:i % 2 + 1], A.is_equal, A.mult), "dg")
+    wait("v", "ds", 2)
+    inc(V.memset(T.ds[:, :, 8::8], 0.0), "dg")
+    DG = cnt["dg"]
+    for _ in digits(0):
         pass
-    if d == 0:
-        inc(V.memset(T.tab0[:, 3 * K:H], EMPTY), "tv")
-        inc(V.memset(T.tab1[:, 0:K], EMPTY), "tv")
-        inc(V.memset(T.tab1[:, 2 * K:3 * K], EMPTY), "tv")
+    if early:
+        inc(V.memset(T.tabs[:, S1:G0], float(EMPTY)), "tw")
+        vfill(6 * K, 7 * K)
+    else:
+        for r in order:
+            low(r, "pk")
+    for i, _ in enumerate(keys(0)):
+        vfill(7 * K + 352 * i, min(8 * K, 7 * K + 352 * (i + 1)))
+    for _ in lists(0, 1, "ko0"):
+        pass
     TV = cnt["tv"]
-    rest = [r for r in range(1, N) if r != d]
+    rest = [r for r in range(1, N) if early or r != d]
 
-    items = ([(d, 0, 8)] if d != 0 else []) + [(0, 0, 3), (0, 3, 8)] + [(r, 0, 8) for r in rest]
+    items = ([] if early else [(d, 0, 4)]) + [(0, 0, 2), (0, 2, 4)] + [(r, 0, 4) for r in rest]
+    vpb = [T.vp0, T.vp1, T.vp2, T.vp3]
+    bank_of = [T.rp1 if (r, q0) == (0, 0) else vpb[r] for r, q0, q1 in items]
     need = {}
-    for i, (r, u0, u1) in enumerate(items):
-        for u in range(u0, u1):
-            need[8 * r + u] = i
+    for i, (r, q0, q1) in enumerate(items):
+        for u in range(2 * q0, 2 * q1):
+            need[8 * r + u] = (i, (u // 2 - q0) // CQ + 1)
+    i0 = need[0][0]
 
-    def keysum(r, kp, slot, name):
-        have("p", r)
+    def keysum(r):
+        kp, slot = KP[r]
         if r > 0:
             have("p", r - 1)
-        for e in range(2):
-            out = kp[:, slot, :, e, :]
-            one = kp[:, slot, 0, e, 0:1]
-            pa, pb, na, nb = T.dg[:, 2 * e, :], T.dg[:, 2 * e + 1, :], T.dg[:, 4 + 2 * e, :], T.dg[:, 5 + 2 * e, :]
-            p0, n0 = T.d0[:, e, :], T.d0[:, 2 + e, :]
-            ms = [(out, pb, dig(r, 0, e, 2, W)), (out, pa, dig(r, 0, e, 1, W - 1)),
-                  (out, nb, dig(r, 1, e, 2, W)), (out, na, dig(r, 1, e, 1, W - 1)),
-                  (one, n0, dig(r, 0, e, 1, 2)), (one, p0, dig(r, 1, e, 1, 2))]
-            if r > 0:
-                ms += [(one, p0, dig(r - 1, 0, e, 1, 2)), (one, n0, dig(r - 1, 1, e, 1, 2))]
-            for i, (o, l, x) in enumerate(ms):
-                ins = PE.matmul(o, l, x, i == 0, i == len(ms) - 1)
-            inc(ins, name)
+        ms = []
+        for j in range(2):
+            for e in range(2):
+                out, one = kp[:, slot, :, e, :], kp[:, slot, 0, e, 0:1]
+                for h in range(2):
+                    ms.append((j, out, T.dg[:, 2 * e + 1, 2 - h:130 - h], dig(r, j, R * h, R * h + R)))
+                    ms.append((j, out, T.dg[:, 2 * e, 2 - h:130 - h], dig(r, j, R * h - 1, R * h + R - 1)))
+                ms.append((j, one, T.ds[:, e, 0:128], dig(r, j, QW - 1)))
+                if r > 0:
+                    ms.append((j, one, T.dw[:, e, 8:136], dig(r - 1, j, QW - 1)))
+        for i, (j, o, l, x) in enumerate(ms):
+            have("p", r, j)
+            ins = PE.matmul(o, l, x, i == 0, i == len(ms) - 1)
+        inc(ins, "kp%d" % r)
 
     def spread(i):
-        r, u0, u1 = items[i]
-        bank = vpb[i % 4]
-        if i >= 4:
-            wait("p", "vc%d" % (i - 4), 1)
-        wait("p", "ge", 4)
-        wait("p", "gct", 2)
+        r, q0, q1 = items[i]
+        bank = bank_of[i]
+        wait("p", "ge", 1)
+        wait("p", "gct", 2 if q1 == 2 else 4)
         wait("p", "cs_m", CSM)
         have("p", r)
-        PE.matmul(bank[:, 0:R * (u1 - u0)], T.cm[0:65, r, :], T.ct[0:65, R * u0:R * u1], True, False)
-        for u in range(u0, u1):
-            for e in range(2):
-                for j in range(2):
-                    o = 17 - 16 * e - j
-                    last = u == u1 - 1 and e == 1 and j == 1
-                    ins = PE.matmul(bank[:, R * (u - u0):R * (u - u0 + 1)], T.em[:, u, o:o + 128], dig(r, j, e, 2, W), False, last)
+        PE.matmul(bank[:, 0:QW * (q1 - q0)], T.cm[0:65, r, :], T.ct[0:65, QW * q0:QW * q1], True, False)
+        for q in range(q0, q1):
+            for j in range(2):
+                ins = PE.matmul(bank[:, QW * (q - q0):QW * (q - q0 + 1)], T.em[:, q, 1 - j:129 - j], dig(r, j), False,
+                                q == q1 - 1 and j == 1)
         inc(ins, "vp%d" % i)
 
-    i0 = 0
-    if d != 0:
+    if not early:
         spread(0)
-        i0 = 1
-    wait("p", "dg", 12)
-    keysum(0, T.kp0, 0, "kp0")
+    wait("p", "dg", DG)
+    keysum(0)
     spread(i0)
     spread(i0 + 1)
-    keysum(1, T.kp1, 0, "kp1")
-    later = list(range(i0 + 2, 5))
-    if d != 1:
-        spread(later.pop(0))
-    wait("p", "k0", 7)
-    keysum(2, T.kp0, 0, "kp2")
-    keysum(3, T.kp0, 1, "kp2")
-    for i in later:
-        spread(i)
-    wait("p", "gf", 8)
-    wait("p", "gi", 1)
-    for k, (r, c0, c) in enumerate(PIECES):
-        bank, n = (T.rp0, T.rp1)[k % 2], c // 2
+    item = {r: i for i, (r, q0, q1) in enumerate(items) if r in rest}
+    keysum(1)
+    spread(item[1])
+    wait("p", "k0", 1)
+    keysum(2)
+    wait("p", "k1", 1)
+    keysum(3)
+    if d != 2:
+        spread(item[2])
+    parts = [max(1, nt // 4) for t0, nt in PIECES]
+
+    def together(k):
+        t0, nt = PIECES[k]
+        bank, n = (T.rp0, T.rp1)[k % 2], 32 * nt
         if k >= 2:
-            wait("p", "ev%d" % (k - 2), 1)
-        for part in range(2):
-            b = TT * r + c0 + part * n
-            for i, s in enumerate((0, 2, 1, 3)):
-                wait("p", "ch%d" % s, 2 * ((b + n) // R - 1))
-                o = 70 - 64 * part - 2 * s
-                ins = PE.matmul(bank[:, 0:n], T.fm[:, s, o:o + 128], T.got[:, s, b:b + n], i == 0 and part == 0, i == 3 and part == 1)
+            wait("p", "ev%d" % (k - 2), parts[k - 2])
+        ms = [(part, s) for part in range(2) for s in (0, 2, 1, 3)]
+        if nt == 1:
+            ms.sort(key=lambda x: x[1] % 2)
+        for i, (part, s) in enumerate(ms):
+            c = R * t0 + part * n
+            wait("p", "ch%d" % s, 2 * ((c + n - 1) // R))
+            o = FZ - 2 * s - part
+            ins = PE.matmul(bank[:, 0:n], T.fm[:, s, o:o + 128], T.got[:, s, c:c + n], i == 0, i == 7)
         inc(ins, "rp%d" % k)
 
-    def offs(s, t):
-        c = 128 * (t // 8) + 32 * s + 4 * (t % 8)
-        return T.off[:, c:c + 4]
+    wait("p", "gf", 4)
+    wait("p", "gi", 1)
+    wait("p", "vc%d" % i0, 1)
+    together(0)
+    if d != 3:
+        spread(item[3])
+    for k in range(1, len(PIECES)):
+        together(k)
 
-    def scatter(q, s, t):
-        wait(q, "vc%d" % need[t], 1)
-        wait(q, "vc%d" % need[t + 1], 1)
-        wait(q, "ch%d" % s, 2 * t)
-        out, src = tab[s][:, 0:H].indirect(offs(s, t)), T.val[:, R * t + 1:R * t + R + 1]
-        inc(V.tensor_copy(out, src) if q == "v" else SC.activation(out, src, F.Silu), "ch%d" % s)
-
-    def gather(q, s, t):
-        if t >= 8:
-            wait(q, "k1", 7)
-        if t >= 16:
-            wait(q, "k2", 7)
-        wait(q, "ch%d" % s, 2 * t - 1)
-        out, src = T.got[:, s, R * t:R * t + R], tab[s][:, 0:H].indirect(offs(s, t))
-        inc(V.tensor_copy(out, src) if q == "v" else SC.activation(out, src, F.Identity), "ch%d" % s)
+    def step(q, kind, s, t):
+        ch, c = "ch%d" % s, 128 * (t // 8) + 32 * s + 4 * (t % 8)
+        win = (T.tabv, T.tabs)[s // 2][:, s % 2 * H:s % 2 * H + H].indirect(T.off[:, c:c + 4])
+        wait(q, "ko%d" % min(t // 8, 2), 4)
+        if kind == "s":
+            for i, n in (need[t], need[t + 1]):
+                wait(q, "vc%d" % i, n)
+        wait(q, ch, cnt.get(ch, 0))
+        if kind == "s":
+            src = T.val[:, R * t + 1:R * t + R + 1]
+            inc(V.tensor_copy(win, src) if q == "v" else SC.activation(win, src, F.Silu), ch)
+        else:
+            out = T.got[:, s, R * t:R * t + R]
+            inc(V.tensor_copy(out, win) if q == "v" else SC.activation(out, win, F.Identity), ch)
 
     def evac(k):
-        r, c0, c = PIECES[k]
-        wait("v", "eb", 3)
-        wait("v", "rp%d" % k, 1)
-        out = (T.land if r == d else T.outb)[:, r, c0 // 2:(c0 + c) // 2]
-        inc(V.tensor_scalar(out, (T.rp0, T.rp1)[k % 2][:, 0:c // 2], T.eb[:, 0:1], None, A.add), "ev%d" % k)
+        t0, nt = PIECES[k]
+        r, c0, n = t0 // 8, 32 * (t0 % 8), 32 * nt // parts[k]
+        for c in range(0, 32 * nt, n):
+            wait("v", "eb", 2)
+            wait("v", "rp%d" % k, 1)
+            out = T.outb[:, r, c0 + c:c0 + c + n]
+            inc(V.tensor_scalar(out, (T.rp0, T.rp1)[k % 2][:, c:c + n], T.eb[:, 0:1], None, A.add), "ev%d" % k)
+            yield
 
-    def copy(q, i):
-        r, u0, u1 = items[i]
-        wait(q, "vp%d" % i, 1)
-        out, src = T.val[:, TT * r + R * u0:TT * r + R * u1], vpb[i % 4][:, 0:R * (u1 - u0)]
-        inc(V.tensor_copy(out, src) if q == "v" else SC.activation(out, src, F.Identity), "vc%d" % i)
+    def copy(i, who="s"):
+        r, q0, q1 = items[i]
+        for q in range(q0, q1, CQ):
+            n = min(CQ, q1 - q)
+            wait(who, "vp%d" % i, 1)
+            out, src = T.val[:, TT * r + QW * q:TT * r + QW * (q + n)], bank_of[i][:, QW * (q - q0):QW * (q - q0 + n)]
+            inc(SC.activation(out, src, F.Identity) if who == "s" else V.tensor_copy(out, src), "vc%d" % i)
+            yield
 
-    k1, k2 = keys(1, 2, T.kp1, "kp1", "k1"), keys(2, N, T.kp0, "kp2", "k2")
-    extra = {(5, 0): k1, (5, 1): k1, (6, 0): k1, (6, 1): k1, (12, 0): k2, (12, 1): k2, (13, 0): k2, (13, 1): k2}
-    ev_at = {14: 0, 17: 1, 25: 2, 26: 3, 28: 4, 30: 5}
+    def run(q, work):
+        tabs, todo = (0, 1) if q == "v" else (2, 3), []
+
+        def other(at):
+            new = [(job, both) for t0, job, both in work if t0 == at]
+            todo.extend(new)
+            while todo and (todo[0][1] or new or at % 1 == 0):
+                if next(todo[0][0], 0) is None:
+                    return
+                todo.pop(0)
+
+        for t in range(NR):
+            for s in tabs * (t > 0):
+                step(q, "g", s, t)
+            other(t)
+            for s in tabs * (t < NR - 1):
+                step(q, "s", s, t)
+            other(t + 0.5)
+        for job, both in todo:
+            for _ in job:
+                pass
+
     NS = len(by_scalar)
     wait("v", "tv", TV)
-    wait("v", "c32", 1)
-    wait("v", "ts0", 1)
-    wait("v", "ts", NS)
-    if d != 0:
-        wait("v", "df", DF)
-    wait("v", "k0", 7)
-    for t in range(32):
-        if t == 8 * items[4][0] - 1:
-            copy("v", 4)
-        if t > 0:
-            gather("v", 0, t)
-            gather("v", 1, t)
-        if (t, 0) in extra:
-            next(extra[(t, 0)])
-        if t in ev_at:
-            evac(ev_at[t])
-        if t < 31:
-            scatter("v", 0, t)
-            scatter("v", 1, t)
-        if (t, 1) in extra:
-            next(extra[(t, 1)])
-    evac(6)
+    wait("v", "c32", 2)
+    wait("v", "ts0", 3)
+    wait("v", "dfv", cnt.get("dfv", 0))
+    wait("v", "tw", 1)
+    run("v", [(1, digits(1), True), (3, keys(1), False), (5.5, lists(1, 2, "ko1"), True),
+              (8, keys(2), False), (11, keys(3), False), (13.5, lists(2, N, "ko2"), True)]
+        + [(t, evac(k), k == 2) for k, t in enumerate((16, 18, 25, 26.5, 28, 30, 31, 31))]
+        + [(21, copy(4, "v"), False)] * (d == 1))
 
     wait("s", "c32", 1)
-    inc(SC.activation(T.tab2[:, 0:K], T.tab0[:, 0:K], F.Silu), "ts0")
-    for s, c0, n in by_scalar:
-        inc(SC.activation(tab[s][:, c0:c0 + n], T.tab0[:, 0:n], F.Identity), "ts")
+    inc(SC.activation(T.tabs[:, 0:256], T.tabv[:, 0:256], F.Silu), "ts0")
+    wait("s", "c32", 2)
+    inc(SC.activation(T.tabs[:, 256:K], T.tabv[:, 256:K], F.Identity), "ts0")
+    inc(SC.activation(T.tabs[:, 2 * K:3 * K], T.tabv[:, 0:K], F.Identity), "ts0")
+    wait("s", "ts0", 2)
+    for c in by_scalar:
+        n = min(K, S1 - c)
+        inc(SC.activation(T.tabs[:, c:c + n], T.tabs[:, 0:n], F.Identity), "ts")
+    if not early:
+        inc(SC.activation(T.tabv[:, 6 * K:7 * K], T.tabs[:, 0:K], F.Identity), "tw")
     for i in range(i0 + 1):
-        copy("s", i)
-    cp_at = {2: i0 + 1}
-    for i in range(i0 + 2, 4):
-        cp_at[8 * items[i][0] - 1] = i
-    wait("s", "ts0", 1)
+        for _ in copy(i):
+            pass
+    wait("s", "ts0", 3)
     wait("s", "ts", NS)
     wait("s", "tg", TG)
     wait("s", "df", DF)
-    wait("s", "k0", 7)
-    for t in range(32):
-        if t in cp_at:
-            copy("s", cp_at[t])
-        if t > 0:
-            gather("s", 2, t)
-            gather("s", 3, t)
-        if t < 31:
-            scatter("s", 2, t)
-            scatter("s", 3, t)
+    wait("s", "tw", cnt.get("tw", 0))
+    run("s", [(1, copy(i0 + 1), False)] + [(8 * items[i][0] - 3, copy(i), False) for i in range(i0 + 2, 5 - (d == 1))])
 
     nth = {}
-    for k, (r, c0, c) in enumerate(PIECES):
-        i, n = nth.get(r, 0), c // 2
+    for k, (t0, nt) in enumerate(PIECES):
+        r, c0, n = t0 // 8, 32 * (t0 % 8), 32 * nt
+        i = nth.get(r, 0)
         nth[r] = i + 1
+        land = T["land%d" % max(0, k - N + 2)]
         if r != d:
-            rid, pid, _ = topo.addr(T.cores[r])
-            wait("g", "ev%d" % k, 1)
-            g.remote_dma(T.land[:, d, c0 // 2:c0 // 2 + n], T.outb[:, r, c0 // 2:c0 // 2 + n],
-                         T.sem["res%d" % i], T.sem.sent, pid, rid, topo.mask(core, T.cores[r]))
-            cnt["sent"] += len(topo.engines(core, T.cores[r]))
+            wait("g", "ev%d" % k, parts[k])
+            send(r, T.outb[:, r, c0:c0 + n], land[d], "res%d" % i)
             continue
-        for yz, out in enumerate((T.y, T.z)):
-            q = "s" if (k == len(PIECES) - 1 and yz == 1) else "y"
-            wait(q, "ev%d" % k, 1)
-            wait(q, "res%d" % i, sum(len(topo.engines(T.cores[w], core)) for w in others))
-            for part in range(2):
-                p0 = 64 * part + 32 * yz
-                inc(Q[q].dma_start(out[:, c0 + part * n:c0 + part * n + n], T.land[p0:p0 + 32, :, c0 // 2:c0 // 2 + n]),
-                    "sta" if q == "y" else "stb", 16)
+        for own in (True, False):
+            for yz, out in enumerate((T.y, T.z)):
+                q = "s" if (k == len(PIECES) - 1 and yz == 1) else "y"
+                name = "sta" if q == "y" else "stb"
+                if own:
+                    wait(q, "ev%d" % k, parts[k])
+                    inc(Q[q].dma_start(out[32 * d:32 * d + 32, 2 * c0:2 * (c0 + n)], T.outb[64 * yz:64 * yz + 64, d, c0:c0 + n]), name, 16)
+                    continue
+                wait(q, "res%d" % i, sum(arr.values()))
+                for a, b in ((0, d), (d + 1, N)):
+                    if a < b:
+                        inc(Q[q].dma_start(out[32 * a:32 * b, 2 * c0:2 * (c0 + n)], land[a:b, 64 * yz:64 * yz + 64, :]), name, 16)
     wait("g", "sent", cnt["sent"])
     wait("y", "sta", cnt["sta"])
     if "stb" in cnt:

from concourse.bass import DstId, RemoteDMATransfer
from concourse.mybir import AluOpType, ActivationFunctionType

N, TT, R, H, S = 4, 512, 64, 4096, 8
NR = N * TT // R
QW = 128
Z = 8
W = Z + QW
EW, DW, FW, FZ = 130, 136, 136, 7
K = 1024
EMPTY, LIFT = 48, 32
CQ = 2
PIECES = [(0, 8), (8, 8), (16, 8), (24, 2), (26, 2), (28, 2), (30, 1), (31, 1)]

SCRATCH = {
    "xq": ("sbuf", [128, N, QW], "int32"),
    "xu": ("sbuf", [128, N, QW], "uint16"),
    "xl": ("sbuf", [128, N, QW], "uint16"),
    "xf": ("sbuf", [128, N, QW], "float32"),
    "hs": ("sbuf", [128, N, 2, W], "bfloat16"),
    "hd": ("sbuf", [128, N, 2, W], "bfloat16"),
    "ds": ("sbuf", [128, 2, DW], "float16"),
    "dw": ("sbuf", [128, 2, DW], "float16"),
    "hq": ("sbuf", [128, 2], "int32"),
    "hf": ("sbuf", [128, 2], "float32"),
    "dk": ("sbuf", [128, DW], "bfloat16"),
    "dg": ("sbuf", [128, 4, DW], "float16"),
    "em": ("sbuf", [128, 4, EW], "bfloat16"),
    "fm": ("sbuf", [128, 4, FW], "bfloat16"),
    "cm": ("sbuf", [128, N, 128], "bfloat16"),
    "ct": ("sbuf", [128, TT], "bfloat16"),
    "eb": ("sbuf", [128, 1], "float32"),
    "kt": ("sbuf", [128, TT], "float32"),
    "ki": ("sbuf", [128, TT], "int32"),
    "kj": ("sbuf", [128, N, 4, 32], "int32"),
    "off": ("sbuf", [128, TT], "uint16"),
    "val": ("sbuf", [128, N * TT], "float32"),
    "tabv": ("sbuf", [128, 2 * H], "bfloat16"),
    "tabs": ("sbuf", [128, 2 * H], "float32"),
    "got": ("sbuf", [128, 4, N * TT], "bfloat16"),
    "outb": ("sbuf", [128, N, 256], "float32"),
    "land0": ("dram", [N, 128, 256], "float32"),
    "land1": ("dram", [N, 128, 64], "float32"),
    "land2": ("dram", [N, 128, 64], "float32"),
    "land3": ("dram", [N, 128, 64], "float32"),
    "land4": ("dram", [N, 128, 32], "float32"),
    "land5": ("dram", [N, 128, 32], "float32"),
    "kp0": ("psum", [128, 4, 4, 2, 16], "float32"),
    "kp1": ("psum", [128, 4, 4, 2, 16], "float32"),
    "vp0": ("psum", [128, 512], "float32"),
    "vp1": ("psum", [128, 512], "float32"),
    "vp2": ("psum", [128, 512], "float32"),
    "vp3": ("psum", [128, 512], "float32"),
    "rp0": ("psum", [128, 512], "float32"),
    "rp1": ("psum", [128, 512], "float32"),
}
SEMAPHORES = (["tw", "dfv", "ld0", "ld1", "ld2", "ld3", "ds", "dz", "ldh", "cz", "fz", "c32", "xz", "kz", "gk", "ge", "gf", "gct", "cs_z", "cs_m", "tv", "ts", "ts0", "tg",
               "df", "hf", "dg", "gi", "eb", "dig0", "dig1", "dig2", "dig3", "pk", "sent", "sta", "stb"]
              + ["kp%d" % i for i in range(N)] + ["k%d" % i for i in range(N)] + ["ko%d" % i for i in range(3)]
              + ["ch%d" % i for i in range(4)] + ["arr%d" % i for i in range(N)]
              + ["vp%d" % i for i in range(5)] + ["vc%d" % i for i in range(5)]
              + ["rp%d" % i for i in range(len(PIECES))] + ["ev%d" % i for i in range(len(PIECES))]
              + ["res%d" % i for i in range(5)])


def rank_program(g, core, T, topo):
    d = T.rank_of(core)
    if d is None:
        return
    A, F = AluOpType, ActivationFunctionType
    V, SC, PE, SY = g.vector, g.scalar, g.tensor, g.sync
    Q = {"g": g, "v": V, "s": SC, "p": PE, "y": SY}
    cnt, seen, top = {}, {}, {}

    def inc(ins, name, n=1):
        ins.then_inc(T.sem[name], n)
        cnt[name] = cnt.get(name, 0) + n

    def wait(q, name, n):
        if seen.get((q, name), 0) < n:
            Q[q].wait_ge(T.sem[name], n)
            seen[(q, name)] = n
            top[name] = max(top.get(name, 0), n)

    def iota(out, pattern, base, step, name):
        inc(g.iota(out, pattern, base, step, allow_small_or_imprecise_dtypes=True), name)

    def fill(out, n, value, name):
        iota(out, [[0, n]], value, 0, name)

    others = [r for r in range(N) if r != d]
    early = d < 2
    order = others if d != 1 else [0, 3, 2]

    def send(r, src, dst, sem):
        rid, pid, _ = topo.addr(T.cores[r])
        g.remote_dma(dst, src, T.sem[sem], T.sem.sent, pid, rid, topo.mask(core, T.cores[r]))
        cnt["sent"] = cnt.get("sent", 0) + len(topo.engines(core, T.cores[r]))

    def deal():
        for i, r in enumerate(order):
            wait("g", "pk", i + 1)
            if early:
                send(r, T.xu[:, r, :], T.xl[:, d, :], "arr%d" % d)
            else:
                send(r, T.hs[:, r, :, :], T.hd[:, d, :, :], "arr%d" % d)

    arr = {r: len(topo.engines(T.cores[r], core)) for r in others}

    def have(q, r, j=1):
        if r > 1 and r != d:
            wait(q, "arr%d" % r, arr[r])
        else:
            wait(q, "dig%d" % r, 1 if j == 0 else 2 if r == d else 3)

    def dig(r, j, c0=0, c1=QW):
        return (T.hs if r == d and not early else T.hd)[:, r, j, Z + c0:Z + c1]

    for i, r in enumerate(order + [d] if early else [d] + order):
        inc((SY, SC)[i % 2].dma_start(T.xq[:, r, :], T.x[32 * r:32 * r + 32, :]), "ld%d" % r, 16)
    for q in range(4):
        inc(SY.dma_start(T.hq[q::4, :], T.hc[32 * d:32 * d + 32, :]), "ldh", 16)
    LDH = cnt["ldh"]

    wait("g", "kz", 1)
    iota(T.dk[:, 2:130:2], [[-32, 4], [-4, 4], [-1, 4]], 0, 1, "gk")
    wait("g", "cz", 1)
    v = T.em[:, :, 1:129:4]
    inc(g.affine_select(v, v, [[-1, 4], [-4, 32]], A.not_equal, 1.0, 0, 1), "ge")
    if early:
        deal()
    wait("g", "ge", 1)
    for u0, u1 in ((0, 4), (4, 8)):
        iota(T.ct[32:64, R * u0:R * u1], [[1, u1 - u0], [0, R]], EMPTY + u0, 0, "gct")
        iota(T.ct[0:32, R * u0:R * u1], [[0, u1 - u0], [1, R]], EMPTY, 0, "gct")
    wait("g", "gct", 3)
    G0 = 7 * K + 512 if early else 6 * K
    fill(T.tabs[:, G0:8 * K], 8 * K - G0, EMPTY, "tg")
    TG = cnt["tg"]
    if not early:
        wait("g", "arr0", arr[0])
        deal()
    first_sent = cnt["sent"]
    fill(T.fm[:, :, :], 4 * FW, 0, "fz")
    fill(T.got[:, :, 0:R], 4 * R, EMPTY, "gi")
    fill(T.eb[0:64, :], 1, -(65 * EMPTY + 1), "eb")
    wait("g", "fz", 1)
    fy, fz = T.fm[:, :, FZ:FZ + 64:8], T.fm[:, :, FZ + 64:FZ + 128:8]
    for step in range(2):
        wait("g", "gf", 2 * step)
        inc(g.affine_select(fy, fy, [[0, 4], [-16, 8]], A.not_equal, (64.0, 1.0)[step], -2 - step, 1), "gf")
        inc(g.affine_select(fz, fz, [[-4, 4], [-16, 8]], A.not_equal, 1.0, -step, 1), "gf")
    wait("g", "gf", 4)
    fill(T.eb[64:128, :], 1, -(2 * EMPTY + 1), "eb")

    S1 = (6 * K + 512, 7 * K, 5 * K, 5 * K)[d]
    by_scalar, by_dma = range(3 * K, S1, K), [1] if early else [1, 5]
    wait("y", "c32", 2)
    for i in (4, 5):
        inc(SY.dma_start(T.tabv[:, i * K:(i + 1) * K], T.tabv[:, 0:K]), "dfv", 16)
    if early:
        wait("y", "sent", first_sent)
    wait("y", "ts0", 2)
    for i in by_dma:
        inc(SY.dma_start(T.tabs[:, i * K:(i + 1) * K], T.tabs[:, 0:K]), "df", 16)
    DF = cnt.get("df", 0)

    KP = [(T.kp0, 0), (T.kp1, 0), (T.kp0, 0), (T.kp1, 0)]

    def keys(r):
        kp, slot = KP[r]
        c0, c1, name = 128 * r, 128 * r + 128, "k%d" % r
        wait("v", "kp%d" % r, 1)
        inc(V.transpose(T.kt[:, c0:c1], kp[:, slot, :, :, :]), name)
        yield
        wait("v", name, 1)
        inc(V.tensor_copy(T.ki[:, c0:c1], T.kt[:, c0:c1]), name)
        yield
        wait("v", name, 2)
        inc(V.tensor_scalar(T.kj[:, r, :, :], T.ki[:, c0:c1], S, H - 1, A.logical_shift_right, A.bitwise_and), name)
        yield

    def lists(r0, r1, name):
        for c in range(4):
            for r in range(r0, r1):
                wait("v", "k%d" % r, 3)
            inc(V.tensor_copy(T.off[:, 128 * r0 + c:128 * r1:4], T.kj[:, r0:r1, c, :]), name)
            yield

    def vfill(c0, c1, name="tv"):
        inc(V.memset(T.tabv[:, c0:c1], float(EMPTY)), name)

    def pack(i):
        wait("v", "ld%d" % order[i], 16)
        inc(V.tensor_copy(T.xu[:, order[i], :], T.xq[:, order[i], :]), "pk")

    def digits(r):
        if r != d:
            name = "dig%d" % r
            wait("v", "arr%d" % r, arr[r])
            inc(V.tensor_scalar(dig(r, 0), T.xl[:, r, :], float(LIFT), None, A.add), name)
            inc(V.tensor_copy(T.xf[:, r, :], T.xl[:, r, :]), name)
            yield
            wait("v", name, 2)
            inc(V.tensor_tensor_scan(dig(r, 1), T.xf[:, r, :], dig(r, 0), 0.0, A.max, A.subtract), name)
            yield

    def low(r, name):
        out = dig(d, 1) if r == d else T.hs[:, r, 1, Z:W]
        inc(V.tensor_tensor(out, T.xq[:, r, :], dig(d, 0) if r == d else T.hs[:, r, 0, Z:W], A.subtract), name)

    vfill(0, 256, "c32")
    inc(V.memset(T.dk[:, :], 200.0), "kz")
    inc(V.memset(T.em[:, :, :], 0.0), "cz")
    vfill(256, K, "c32")
    inc(V.memset(T.hd[:, 0:2, :, 0:Z], 0.0), "xz")
    if not early:
        inc(V.memset(T.hs[:, :, :, 0:Z], 0.0), "xz")
    inc(V.memset(T.cm[:, :, :], 0.0), "cs_z")
    inc(V.memset(T.dw[:, :, :], 0.0), "dz")
    if early:
        pack(0)
    wait("v", "cs_z", 1)
    inc(V.memset(T.cm[0:1, :, 3::16], 1.0), "cs_m")
    inc(V.memset(T.cm[32:33, :, 2::16], 1.0), "cs_m")
    inc(V.memset(T.cm[64:65, :, 1::4], 2.0 * EMPTY + 1), "cs_m")
    if early:
        pack(1)
    for r in range(1, N):
        inc(V.memset(T.cm[64:65, r, 2::16], 8.0 * r), "cs_m")
    if early:
        pack(2)
    inc(V.memset(T.ct[64:65, :], 1.0), "cs_m")
    CSM = cnt["cs_m"]
    vfill(K, 2 * K)
    if early:
        wait("v", "ld%d" % d, 16)
        inc(V.tensor_scalar(dig(d, 0), T.xq[:, d, :], float(LIFT), None, A.add), "dig%d" % d)
    else:
        for r in range(N):
            wait("v", "ld%d" % r, 16)
        inc(V.tensor_scalar(T.hs[:, :, 0, Z:W], T.xq[:, :, :], float(LIFT), None, A.add), "dig%d" % d)
    vfill(2 * K, 3 * K)
    wait("v", "dig%d" % d, 1)
    low(d, "dig%d" % d)
    wait("v", "ldh", LDH)
    inc(V.tensor_copy(T.hf[:, :], T.hq[:, :]), "hf")
    vfill(3 * K, 4 * K)
    wait("v", "hf", 1)
    wait("v", "gk", 1)
    wait("v", "dz", 1)
    wait("v", "xz", cnt["xz"])
    for e in range(2):
        inc(V.tensor_scalar(T.ds[:, e, :], T.dk[:, :], 16.0 * e, T.hf[:, 0:1], A.is_equal, A.mult), "ds")
        inc(V.tensor_scalar(T.dw[:, e, 8::8], T.dk[:, 8::8], 16.0 * e, T.hf[:, 0:1], A.is_equal, A.mult), "dg")
    for i in range(4):
        inc(V.tensor_scalar(T.dg[:, i, :], T.dk[:, :], 16.0 * (i // 2), T.hf[:, i % 2:i % 2 + 1], A.is_equal, A.mult), "dg")
    wait("v", "ds", 2)
    inc(V.memset(T.ds[:, :, 8::8], 0.0), "dg")
    DG = cnt["dg"]
    for _ in digits(0):
        pass
    if early:
        inc(V.memset(T.tabs[:, S1:G0], float(EMPTY)), "tw")
        vfill(6 * K, 7 * K)
    else:
        for r in order:
            low(r, "pk")
    for i, _ in enumerate(keys(0)):
        vfill(7 * K + 352 * i, min(8 * K, 7 * K + 352 * (i + 1)))
    for _ in lists(0, 1, "ko0"):
        pass
    TV = cnt["tv"]
    rest = [r for r in range(1, N) if early or r != d]

    items = ([] if early else [(d, 0, 4)]) + [(0, 0, 2), (0, 2, 4)] + [(r, 0, 4) for r in rest]
    vpb = [T.vp0, T.vp1, T.vp2, T.vp3]
    bank_of = [T.rp1 if (r, q0) == (0, 0) else vpb[r] for r, q0, q1 in items]
    need = {}
    for i, (r, q0, q1) in enumerate(items):
        for u in range(2 * q0, 2 * q1):
            need[8 * r + u] = (i, (u // 2 - q0) // CQ + 1)
    i0 = need[0][0]

    def keysum(r):
        kp, slot = KP[r]
        if r > 0:
            have("p", r - 1)
        ms = []
        for j in range(2):
            for e in range(2):
                out, one = kp[:, slot, :, e, :], kp[:, slot, 0, e, 0:1]
                for h in range(2):
                    ms.append((j, out, T.dg[:, 2 * e + 1, 2 - h:130 - h], dig(r, j, R * h, R * h + R)))
                    ms.append((j, out, T.dg[:, 2 * e, 2 - h:130 - h], dig(r, j, R * h - 1, R * h + R - 1)))
                ms.append((j, one, T.ds[:, e, 0:128], dig(r, j, QW - 1)))
                if r > 0:
                    ms.append((j, one, T.dw[:, e, 8:136], dig(r - 1, j, QW - 1)))
        for i, (j, o, l, x) in enumerate(ms):
            have("p", r, j)
            ins = PE.matmul(o, l, x, i == 0, i == len(ms) - 1)
        inc(ins, "kp%d" % r)

    def spread(i):
        r, q0, q1 = items[i]
        bank = bank_of[i]
        wait("p", "ge", 1)
        wait("p", "gct", 2 if q1 == 2 else 4)
        wait("p", "cs_m", CSM)
        have("p", r)
        PE.matmul(bank[:, 0:QW * (q1 - q0)], T.cm[0:65, r, :], T.ct[0:65, QW * q0:QW * q1], True, False)
        for q in range(q0, q1):
            for j in range(2):
                ins = PE.matmul(bank[:, QW * (q - q0):QW * (q - q0 + 1)], T.em[:, q, 1 - j:129 - j], dig(r, j), False,
                                q == q1 - 1 and j == 1)
        inc(ins, "vp%d" % i)

    if not early:
        spread(0)
    wait("p", "dg", DG)
    keysum(0)
    spread(i0)
    spread(i0 + 1)
    item = {r: i for i, (r, q0, q1) in enumerate(items) if r in rest}
    keysum(1)
    spread(item[1])
    wait("p", "k0", 1)
    keysum(2)
    wait("p", "k1", 1)
    keysum(3)
    if d != 2:
        spread(item[2])
    parts = [max(1, nt // 4) for t0, nt in PIECES]

    def together(k):
        t0, nt = PIECES[k]
        bank, n = (T.rp0, T.rp1)[k % 2], 32 * nt
        if k >= 2:
            wait("p", "ev%d" % (k - 2), parts[k - 2])
        ms = [(part, s) for part in range(2) for s in (0, 2, 1, 3)]
        if nt == 1:
            ms.sort(key=lambda x: x[1] % 2)
        for i, (part, s) in enumerate(ms):
            c = R * t0 + part * n
            wait("p", "ch%d" % s, 2 * ((c + n - 1) // R))
            o = FZ - 2 * s - part
            ins = PE.matmul(bank[:, 0:n], T.fm[:, s, o:o + 128], T.got[:, s, c:c + n], i == 0, i == 7)
        inc(ins, "rp%d" % k)

    wait("p", "gf", 4)
    wait("p", "gi", 1)
    wait("p", "vc%d" % i0, 1)
    together(0)
    if d != 3:
        spread(item[3])
    for k in range(1, len(PIECES)):
        together(k)

    def step(q, kind, s, t):
        ch, c = "ch%d" % s, 128 * (t // 8) + 32 * s + 4 * (t % 8)
        win = (T.tabv, T.tabs)[s // 2][:, s % 2 * H:s % 2 * H + H].indirect(T.off[:, c:c + 4])
        wait(q, "ko%d" % min(t // 8, 2), 4)
        if kind == "s":
            for i, n in (need[t], need[t + 1]):
                wait(q, "vc%d" % i, n)
        wait(q, ch, cnt.get(ch, 0))
        if kind == "s":
            src = T.val[:, R * t + 1:R * t + R + 1]
            inc(V.tensor_copy(win, src) if q == "v" else SC.activation(win, src, F.Silu), ch)
        else:
            out = T.got[:, s, R * t:R * t + R]
            inc(V.tensor_copy(out, win) if q == "v" else SC.activation(out, win, F.Identity), ch)

    def evac(k):
        t0, nt = PIECES[k]
        r, c0, n = t0 // 8, 32 * (t0 % 8), 32 * nt // parts[k]
        for c in range(0, 32 * nt, n):
            wait("v", "eb", 2)
            wait("v", "rp%d" % k, 1)
            out = T.outb[:, r, c0 + c:c0 + c + n]
            inc(V.tensor_scalar(out, (T.rp0, T.rp1)[k % 2][:, c:c + n], T.eb[:, 0:1], None, A.add), "ev%d" % k)
            yield

    def copy(i, who="s"):
        r, q0, q1 = items[i]
        for q in range(q0, q1, CQ):
            n = min(CQ, q1 - q)
            wait(who, "vp%d" % i, 1)
            out, src = T.val[:, TT * r + QW * q:TT * r + QW * (q + n)], bank_of[i][:, QW * (q - q0):QW * (q - q0 + n)]
            inc(SC.activation(out, src, F.Identity) if who == "s" else V.tensor_copy(out, src), "vc%d" % i)
            yield

    def run(q, work):
        tabs, todo = (0, 1) if q == "v" else (2, 3), []

        def other(at):
            new = [(job, both) for t0, job, both in work if t0 == at]
            todo.extend(new)
            while todo and (todo[0][1] or new or at % 1 == 0):
                if next(todo[0][0], 0) is None:
                    return
                todo.pop(0)

        for t in range(NR):
            for s in tabs * (t > 0):
                step(q, "g", s, t)
            other(t)
            for s in tabs * (t < NR - 1):
                step(q, "s", s, t)
            other(t + 0.5)
        for job, both in todo:
            for _ in job:
                pass

    NS = len(by_scalar)
    wait("v", "tv", TV)
    wait("v", "c32", 2)
    wait("v", "ts0", 3)
    wait("v", "dfv", cnt.get("dfv", 0))
    wait("v", "tw", 1)
    run("v", [(1, digits(1), True), (3, keys(1), False), (5.5, lists(1, 2, "ko1"), True),
              (8, keys(2), False), (11, keys(3), False), (13.5, lists(2, N, "ko2"), True)]
        + [(t, evac(k), k == 2) for k, t in enumerate((16, 18, 25, 26.5, 28, 30, 31, 31))]
        + [(21, copy(4, "v"), False)] * (d == 1))

    wait("s", "c32", 1)
    inc(SC.activation(T.tabs[:, 0:256], T.tabv[:, 0:256], F.Silu), "ts0")
    wait("s", "c32", 2)
    inc(SC.activation(T.tabs[:, 256:K], T.tabv[:, 256:K], F.Identity), "ts0")
    inc(SC.activation(T.tabs[:, 2 * K:3 * K], T.tabv[:, 0:K], F.Identity), "ts0")
    wait("s", "ts0", 2)
    for c in by_scalar:
        n = min(K, S1 - c)
        inc(SC.activation(T.tabs[:, c:c + n], T.tabs[:, 0:n], F.Identity), "ts")
    if not early:
        inc(SC.activation(T.tabv[:, 6 * K:7 * K], T.tabs[:, 0:K], F.Identity), "tw")
    for i in range(i0 + 1):
        for _ in copy(i):
            pass
    wait("s", "ts0", 3)
    wait("s", "ts", NS)
    wait("s", "tg", TG)
    wait("s", "df", DF)
    wait("s", "tw", cnt.get("tw", 0))
    run("s", [(1, copy(i0 + 1), False)] + [(8 * items[i][0] - 3, copy(i), False) for i in range(i0 + 2, 5 - (d == 1))])

    nth = {}
    for k, (t0, nt) in enumerate(PIECES):
        r, c0, n = t0 // 8, 32 * (t0 % 8), 32 * nt
        i = nth.get(r, 0)
        nth[r] = i + 1
        land = T["land%d" % max(0, k - N + 2)]
        if r != d:
            wait("g", "ev%d" % k, parts[k])
            send(r, T.outb[:, r, c0:c0 + n], land[d], "res%d" % i)
            continue
        for own in (True, False):
            for yz, out in enumerate((T.y, T.z)):
                q = "s" if (k == len(PIECES) - 1 and yz == 1) else "y"
                name = "sta" if q == "y" else "stb"
                if own:
                    wait(q, "ev%d" % k, parts[k])
                    inc(Q[q].dma_start(out[32 * d:32 * d + 32, 2 * c0:2 * (c0 + n)], T.outb[64 * yz:64 * yz + 64, d, c0:c0 + n]), name, 16)
                    continue
                wait(q, "res%d" % i, sum(arr.values()))
                for a, b in ((0, d), (d + 1, N)):
                    if a < b:
                        inc(Q[q].dma_start(out[32 * a:32 * b, 2 * c0:2 * (c0 + n)], land[a:b, 64 * yz:64 * yz + 64, :]), name, 16)
    wait("g", "sent", cnt["sent"])
    wait("y", "sta", cnt["sta"])
    if "stb" in cnt:
        wait("s", "stb", cnt["stb"])
    for name in cnt:
        if top.get(name, 0) < cnt[name]:
            wait("p", name, cnt[name])
